import numpy as np
import ml_dtypes


def mxq(x, axis, fmt="e4m3"):
    dtype, down = {"e4m3": (ml_dtypes.float8_e4m3fn, 7), "e5m2": (ml_dtypes.float8_e5m2, 14)}[fmt]
    v = np.moveaxis(np.asarray(x, np.float32).astype(ml_dtypes.bfloat16).astype(np.float64), axis, -1)
    blocks = v.reshape(v.shape[:-1] + (-1, 32))
    amax = np.abs(blocks).max(-1, keepdims=True)
    byte = np.maximum(np.where(amax > 0, np.frexp(amax)[1] - 1 + 127, 0) - down, 1)
    scale = np.exp2(byte - 127.0)
    codes = (blocks / scale).astype(np.float32).astype(dtype).astype(np.float64)
    return np.moveaxis((codes * scale).reshape(v.shape), -1, axis)


WIDE = False


def mx_kscale(k):
    if not WIDE:
        return np.ones(k)
    levels = np.array([10, -10, 5, -5, 0])
    if k % 512:
        return np.exp2(np.random.permutation(np.resize(levels, k // 32))).repeat(32)
    a = np.empty((k // 512, 16))
    for p in range(k // 512):
        a[p, :8] = np.random.permutation(np.resize(levels, 8))
        for g in range(8):
            far = levels[np.abs(levels - a[p, g]) >= 10]
            a[p, g + 8] = far[np.random.randint(len(far))]
    return np.exp2(a.ravel()).repeat(32)


def f64(x):
    return np.asarray(x).astype(np.float64)


def striped(idx):
    return np.tile(idx.reshape(-1, 16).T, (8, 1)).astype(np.uint16)


def unstriped(offs):
    return offs[:16].T.reshape(-1).astype(np.int64)


def striped8(idx):
    return np.concatenate([x.reshape(-1, 16).T for x in idx]).astype(np.uint16)


def runs(offs, k):
    lists = np.stack([offs[16 * r : 16 * r + 16].T.reshape(-1) for r in range(8)]).astype(np.int64)
    return lists[np.arange(k) % 512 // 64]


def pack_weight(w):
    k, n = w.shape
    w = f64(np.asarray(w, np.float32).astype(ml_dtypes.bfloat16)).reshape(k // 32, 32, n)
    amax = np.abs(w).max(1)
    byte = np.clip(np.where(amax > 0, np.frexp(amax)[1] - 1 + 127 - 7, 1), 1, 254)
    scaled = (w * np.exp2(127.0 - byte)[:, None, :]).reshape(k, n).astype(np.float32)
    words = np.ascontiguousarray(scaled.reshape(k // 512, 128, 4, n).transpose(0, 1, 3, 2)).astype(ml_dtypes.float8_e4m3fn).view(np.uint8)
    return words, np.ascontiguousarray(byte.astype(np.uint8).reshape(k // 512, 16, n))


def unpack_weight(words, scales):
    g, p, n, _ = words.shape
    vals = np.ascontiguousarray(words).view(ml_dtypes.float8_e4m3fn).astype(np.float64) * np.repeat(np.exp2(scales.astype(np.float64) - 127.0), 8, axis=1)[..., None]
    return vals.transpose(0, 1, 3, 2).reshape(g * 512, n)


def sigmoid(v):
    return 1.0 / (1.0 + np.exp(-np.maximum(v, -700.0)))


K, T, S, N, H, W = 512, 2048, 512, 512, 512, 2048


def setup_inputs():
    n = np.random.standard_normal
    s = mx_kscale(K)[:, None]
    u = mx_kscale(S)
    packed_xT = pack_weight(n((K, T)) * s)
    return {
        "x_words": packed_xT[0],
        "x_scales": packed_xT[1],
        "wa": (n((K, H)) / np.sqrt(K) / s).astype(np.float32),
        "wb": (n((K, N)) / np.sqrt(K) / s).astype(np.float32),
        "gt": (np.random.uniform(0.5, 1.5, (S, 1)) * u[:, None]).astype(np.float32),
        "gi": (np.random.uniform(0.5, 1.5, (S, 1)) / u[:, None]).astype(np.float32),
        "offs": striped(np.random.permutation(T)[:S]),
        "two": striped(np.random.permutation(T)[:S]),
        "n1": striped(np.random.randint(0, H, W)),
        "n2": striped(np.random.permutation(N)),
        "n3": striped(np.random.permutation(N)),
        "n4": striped8(np.stack([np.random.permutation(N) for _ in range(8)])),
        "n5": striped8(np.stack([np.random.permutation(N) for _ in range(8)])),
    }


def reference(x_words, x_scales, wa, wb, gt, gi, offs, two, n1, n2, n3, n4, n5):
    xq = unpack_weight(x_words, x_scales)[:, unstriped(offs)]
    a = xq.T @ mxq(f64(wa), 0, "e4m3")
    mb = a[:, unstriped(n1)]
    ms = mb.reshape(S, H, 4).sum(axis=2)
    z = f64(gt) * (a * sigmoid(ms))
    x_two = unpack_weight(x_words, x_scales)[:, unstriped(two)]
    b = x_two.T @ mxq(f64(wb), 0, "e4m3")
    ex = np.exp(b)
    z2 = f64(gi) * (np.log(ex + ex[:, unstriped(n2)]) - b[:, unstriped(n3)])
    cv = 0.0625 * ((mxq(z, 0, "e4m3").T @ mxq(z2, 0, "e4m3")))
    return np.maximum(cv[np.arange(H)[:, None], runs(n4, H)], cv[np.arange(H)[:, None], runs(n5, H)]) - (0.75 * cv)

@@ -1,0 +1,330 @@
+from contextlib import ExitStack
+
+import concourse.mybir as mybir
+
+K, T, S, N, H, W = 512, 2048, 512, 512, 512, 2048
+FLOPS = 2 * (K * S * H + K * S * N + S * H * N)
+
+F32 = mybir.dt.float32
+BF16 = mybir.dt.bfloat16
+I32 = mybir.dt.int32
+U32 = mybir.dt.uint32
+U16 = mybir.dt.uint16
+U8 = mybir.dt.uint8
+FP8X4 = mybir.dt.float8_e4m3fn_x4
+ALU = mybir.AluOpType
+ACT = mybir.ActivationFunctionType
+AX = mybir.AxisListType
+
+P = 128
+PACK = 4
+PAD = 16
+RUNS = 8
+HALF = 256
+
+
+def tile_picked_mombgsumglseover_none_p_kernel(
+    tc, x_words, x_scales, wa, wb, gt, gi, offs, two, n1, n2, n3, n4, n5, out
+):
+    nc = tc.nc
+    with ExitStack() as ctx:
+        held = ctx.enter_context(tc.tile_pool(name="held", bufs=1))
+        psum = ctx.enter_context(tc.psum_pool(name="psum", bufs=1))
+
+        def sb(name, shape, dtype, tag=None):
+            return held.tile(shape, dtype, name=name, tag=tag or name, align_bytes=64)
+
+        def load_list(name, src):
+            tile = sb(name, list(src.shape), U16)
+            nc.sync.dma_start(tile[:], src)
+            return tile
+
+        table_scales = sb("table_scales", [P, T], U8)
+        nc.vector.memset(table_scales[:].bitcast(I32), 0)
+        gi_cols = sb("gi_cols", [P, PACK], F32)
+        nc.gpsimd.dma_start(gi_cols[:], gi.rearrange("(p t) o -> p (t o)", t=PACK))
+        gt_cols = sb("gt_cols", [P, PACK], F32)
+        nc.gpsimd.dma_start(gt_cols[:], gt.rearrange("(p t) o -> p (t o)", t=PACK))
+
+        two_l = load_list("two_l", two)
+        n2_l = load_list("n2_l", n2)
+        table_words = sb("table_words", [P, T], I32)
+        nc.sync.dma_start(table_words[:], x_words[0].rearrange("p c r -> p (c r)").bitcast(I32))
+        for q in range(4):
+            nc.sync.dma_start(
+                table_scales[32 * q : 32 * q + 4, :].bitcast(I32),
+                x_scales[0, 4 * q : 4 * q + 4, :].bitcast(I32),
+            )
+        wb_rows = wb.rearrange("(p j) n -> p j n", j=PACK)
+        wb_raw = []
+        for u in range(2):
+            raw = sb("wb_raw%d" % u, [P, PACK, HALF], F32)
+            nc.sync.dma_start(raw[:], wb_rows[:, :, u * HALF : (u + 1) * HALF])
+            wb_raw.append(raw)
+        wa_raw = sb("wa_raw", [P, PACK, H], F32)
+        nc.sync.dma_start(wa_raw[:], wa.rearrange("(p j) n -> p j n", j=PACK))
+        offs_l = load_list("offs_l", offs)
+        n3_l = load_list("n3_l", n3)
+        n1_l = load_list("n1_l", n1)
+        n4_l = load_list("n4_l", n4)
+        n5_l = load_list("n5_l", n5)
+
+        def window(name):
+            tile = sb(name, [P, N + PAD], F32)
+            nc.gpsimd.memset(tile[:, N:], 0.0)
+            return tile
+
+        ex_win = [window("ex_win%d" % t) for t in range(PACK)]
+        gb_win = [window("gb_win%d" % t) for t in range(PACK)]
+        a_win = [window("a_win%d" % t) for t in range(PACK)]
+
+        def pick_words(name, lst):
+            words = sb(name, [P, S], U32)
+            nc.vector.tensor_copy(
+                words[:].rearrange("p (t m) -> p m t", t=PACK),
+                table_words[:].bitcast(U32).indirect(lst[:]),
+            )
+            return words
+
+        def pick_scales(name, lst):
+            picked = sb(name + "_listed", [P, S], U8)
+            nc.vector.tensor_copy(picked[:], table_scales[:].indirect(lst[:]))
+            dealt = sb(name, [P, S], U8)
+            nc.vector.tensor_copy(
+                dealt[:].rearrange("p (t m) -> p t m", t=PACK),
+                picked[:].rearrange("p (m t) -> p t m", t=PACK),
+            )
+            return dealt
+
+        def weave_views(dst, src):
+            return (
+                dst.rearrange("p (c i t) -> p c t i", i=4, t=PACK),
+                src.rearrange("p t (c i) -> p c t i", i=4),
+            )
+
+        def gather(dst, win, lst):
+            nc.scalar.activation(dst, win.indirect(lst), ACT.Copy)
+
+        def mx_pass(acc, lhs, lhs_scale, rhs, rhs_scale):
+            nc.tensor.matmul_mx(
+                out=acc, lhsT=lhs.bitcast(FP8X4), lhsT_scale=lhs_scale,
+                rhs=rhs.bitcast(FP8X4), rhs_scale=rhs_scale, start=True, stop=True,
+            )
+
+        xb_words = pick_words("xb_words", two_l)
+        xb_scales = pick_scales("xb_scales", two_l)
+        wb_codes = sb("wb_codes", [P, N], U32)
+        wb_scales = sb("wb_scales", [P, N], U8)
+        wb_woven = []
+        for u in range(2):
+            woven = sb("wb_woven%d" % u, [P, PACK * HALF], BF16)
+            dst, src = weave_views(woven[:], wb_raw[u][:])
+            if u == 0:
+                nc.scalar.copy(dst, src)
+            else:
+                nc.vector.tensor_copy(dst, src)
+            wb_woven.append(woven)
+        for u in range(2):
+            cols = slice(u * HALF, (u + 1) * HALF)
+            nc.vector.quantize_mx(wb_codes[:, cols].bitcast(FP8X4), wb_scales[:, cols], wb_woven[u][:])
+        b_acc = []
+        for t in range(PACK):
+            acc = psum.tile([P, N], F32, name="b_acc%d" % t, tag="bank%d" % t)
+            rows = slice(t * P, (t + 1) * P)
+            for u in range(2):
+                cols = slice(u * HALF, (u + 1) * HALF)
+                mx_pass(acc[:, cols], xb_words[:, rows], xb_scales[:, rows], wb_codes[:, cols], wb_scales[:, cols])
+            b_acc.append(acc)
+
+        ex_sum = sb("ex_sum", [P, PACK, N], F32)
+        ex_n2 = [sb("ex_n2_%d" % t, [P, N], F32) for t in range(PACK)]
+
+        def exp_step(t):
+            nc.scalar.activation(ex_win[t][:, :N], b_acc[t][:], ACT.Exp)
+            gather(ex_n2[t][:], ex_win[t][:], n2_l[:])
+            nc.vector.tensor_scalar(gb_win[t][:, :N], b_acc[t][:], gi_cols[:, t : t + 1], None, ALU.mult)
+
+        def add_step(t):
+            nc.vector.tensor_tensor(ex_sum[:, t, :], ex_win[t][:, :N], ex_n2[t][:], ALU.add)
+
+        exp_step(0)
+        xa_words = pick_words("xa_words", offs_l)
+        add_step(0)
+        exp_step(1)
+        xa_scales = pick_scales("xa_scales", offs_l)
+        add_step(1)
+        exp_step(2)
+        wa_woven = sb("wa_woven", [P, PACK * H], BF16)
+        dst, src = weave_views(wa_woven[:], wa_raw[:])
+        nc.vector.tensor_copy(dst, src)
+        add_step(2)
+        exp_step(3)
+        wa_codes = sb("wa_codes", [P, H], U32)
+        wa_scales = sb("wa_scales", [P, H], U8)
+        nc.vector.quantize_mx(wa_codes[:].bitcast(FP8X4), wa_scales[:], wa_woven[:])
+        add_step(3)
+
+        gb_n3 = [sb("gb_n3_%d" % t, [P, N], F32) for t in range(PACK)]
+        for t in range(PACK):
+            gather(gb_n3[t][:], gb_win[t][:], n3_l[:])
+        lse = sb("lse", [P, PACK, N], F32)
+        nc.scalar.activation(lse[:], ex_sum[:], ACT.Ln)
+
+        for t in range(PACK):
+            acc = psum.tile([P, H], F32, name="a_acc%d" % t, tag="bank%d" % (PACK + t))
+            rows = slice(t * P, (t + 1) * P)
+            mx_pass(acc[:], xa_words[:, rows], xa_scales[:, rows], wa_codes[:], wa_scales[:])
+            nc.vector.tensor_copy(a_win[t][:, :H], acc[:])
+
+        z2_rows = sb("z2_rows", [P, PACK, N], BF16)
+        for t in range(PACK):
+            nc.vector.scalar_tensor_tensor(
+                z2_rows[:, t, :], lse[:, t, :], gi_cols[:, t : t + 1], gb_n3[t][:], ALU.mult, ALU.subtract
+            )
+        z2_woven = sb("z2_woven", [P, PACK * N], BF16)
+        dst, src = weave_views(z2_woven[:], z2_rows[:])
+        nc.vector.tensor_copy(dst, src)
+        z2_codes = sb("z2_codes", [P, N], U32)
+        z2_scales = sb("z2_scales", [P, N], U8)
+        nc.vector.quantize_mx(z2_codes[:].bitcast(FP8X4), z2_scales[:], z2_woven[:])
+
+        z_rows = [sb("z_rows%d" % u, [P, PACK, HALF], BF16) for u in range(2)]
+
+        def sum4(dst, src):
+            nc.vector.tensor_reduce(dst, src.rearrange("p (j f) -> p j f", f=4), AX.X, ALU.add)
+
+        def z_step(t, u, sig):
+            nc.vector.scalar_tensor_tensor(
+                z_rows[u][:, t, :].rearrange("p (r k) -> p r k", r=RUNS),
+                a_win[t][:, :H].rearrange("p (r u k) -> p r u k", r=RUNS, u=2)[:, :, u, :],
+                gt_cols[:, t : t + 1], sig, ALU.mult, ALU.mult,
+            )
+
+        def whole_gather(t):
+            mb = sb("mb%d" % t, [P, W], F32)
+            for q in range(4):
+                gather(mb[:, q * 512 : (q + 1) * 512], a_win[t][:], n1_l[:, q * 32 : (q + 1) * 32])
+            return mb
+
+        def whole_sums(t, mb):
+            ms = sb("ms%d" % t, [P, H], F32, tag="hold%d" % t)
+            for q in range(2):
+                sum4(ms[:, q * HALF : (q + 1) * HALF], mb[:, q * 1024 : (q + 1) * 1024])
+            sig = sb("sig%d" % t, [P, H], F32)
+            nc.scalar.activation(sig[:], ms[:], ACT.Sigmoid)
+            return sig[:].rearrange("p (r u k) -> p r u k", r=RUNS, u=2)
+
+        def part_gather(t, u, r0, r1, tag=None):
+            mb = sb("mb%d_%d_%d" % (t, u, r0), [P, (r1 - r0) * 128], F32, tag=tag)
+            for r in range(r0, r1):
+                c0 = 16 * r + 8 * u
+                gather(mb[:, (r - r0) * 128 : (r - r0 + 1) * 128], a_win[t][:], n1_l[:, c0 : c0 + 8])
+            return mb
+
+        def half_ms(t, u):
+            return sb("ms%d_%d" % (t, u), [P, HALF], F32, tag="hold%d_%d" % (t, u))
+
+        def half_sig(t, u, ms):
+            sig = sb("sig%d_%d" % (t, u), [P, HALF], F32)
+            nc.scalar.activation(sig[:], ms[:], ACT.Sigmoid)
+            return sig[:].rearrange("p (r k) -> p r k", r=RUNS)
+
+        cv_win = [sb("cv_win%d" % c, [P, N], F32) for c in range(4)]
+
+        def weave_z(c):
+            u, e = divmod(c, 2)
+            woven = sb("z_woven%d" % c, [P, PACK * P], BF16)
+            nc.vector.tensor_copy(
+                woven[:].rearrange("p (r a i t) -> p r a t i", r=RUNS, a=4, i=4),
+                z_rows[u][:].rearrange("p t (r e a i) -> p e r a t i", r=RUNS, e=2, a=4)[:, e],
+            )
+            return woven
+
+        def cv_product(c, woven):
+            codes = sb("z_codes%d" % c, [P, P], U32)
+            scales = sb("z_scales%d" % c, [P, P], U8)
+            nc.vector.quantize_mx(codes[:].bitcast(FP8X4), scales[:], woven[:])
+            acc = psum.tile([P, N], F32, name="cv_acc%d" % c, tag="bank%d" % c)
+            mx_pass(acc[:], codes[:], scales[:], z2_codes[:], z2_scales[:])
+            return acc
+
+        def cv_out_of_psum(c, acc):
+            nc.vector.tensor_scalar(cv_win[c][:], acc[:], 0.0625, None, ALU.mult)
+
+        g4 = [sb("g4_%d" % c, [P, N], F32) for c in range(4)]
+        g5 = [sb("g5_%d" % c, [P, N], F32) for c in range(4)]
+        top = [sb("top%d" % c, [P, N], F32) for c in range(4)]
+        res = [sb("res%d" % c, [P, N], F32) for c in range(4)]
+        out_rows = out.rearrange("(r c i) n -> c r i n", r=RUNS, c=4)
+
+        def cv_gather(c, v):
+            cols = slice(v * HALF, (v + 1) * HALF)
+            gather(g4[c][:, cols], cv_win[c][:], n4_l[:, 16 * v : 16 * v + 16])
+            gather(g5[c][:, cols], cv_win[c][:], n5_l[:, 16 * v : 16 * v + 16])
+
+        def finish(c, cols):
+            nc.vector.tensor_tensor(top[c][:, cols], g4[c][:, cols], g5[c][:, cols], ALU.max)
+            nc.vector.scalar_tensor_tensor(
+                res[c][:, cols], cv_win[c][:, cols], -0.75, top[c][:, cols], ALU.mult, ALU.add
+            )
+            nc.sync.dma_start(out_rows[c][:, :, cols], res[c][:, cols])
+
+        mb0 = whole_gather(0)
+        mb1 = whole_gather(1)
+        sig0 = whole_sums(0, mb0)
+        mb20 = part_gather(2, 0, 0, 8, tag="hold0")
+        sig1 = whole_sums(1, mb1)
+        z_step(0, 0, sig0[:, :, 0, :])
+        mb30a = part_gather(3, 0, 0, 6, tag="hold1")
+        mb30b = part_gather(3, 0, 6, 8)
+        ms20 = half_ms(2, 0)
+        sum4(ms20[:], mb20[:])
+        sig20 = half_sig(2, 0, ms20)
+        z_step(1, 0, sig1[:, :, 0, :])
+        z_step(0, 1, sig0[:, :, 1, :])
+        z_step(1, 1, sig1[:, :, 1, :])
+        ms30 = half_ms(3, 0)
+        sum4(ms30[:, :192], mb30a[:])
+        z_step(2, 0, sig20)
+        mb21a = part_gather(2, 1, 0, 2, tag="hold2_0")
+        sum4(ms30[:, 192:], mb30b[:])
+        sig30 = half_sig(3, 0, ms30)
+        mb21b = part_gather(2, 1, 2, 8, tag="hold3_0")
+        z_step(3, 0, sig30)
+        woven0 = weave_z(0)
+        woven1 = weave_z(1)
+        acc0 = cv_product(0, woven0)
+        acc1 = cv_product(1, woven1)
+        ms21 = half_ms(2, 1)
+        sum4(ms21[:, :64], mb21a[:])
+        sum4(ms21[:, 64:], mb21b[:])
+        mb31a = part_gather(3, 1, 0, 4)
+        sig21 = half_sig(2, 1, ms21)
+        mb31b = part_gather(3, 1, 4, 8, tag="hold2_1")
+        cv_out_of_psum(0, acc0)
+        ms31 = half_ms(3, 1)
+        sum4(ms31[:, :128], mb31a[:])
+        z_step(2, 1, sig21)
+        cv_gather(0, 0)
+        sum4(ms31[:, 128:], mb31b[:])
+        sig31 = half_sig(3, 1, ms31)
+        cv_out_of_psum(1, acc1)
+        cv_gather(0, 1)
+        z_step(3, 1, sig31)
+        woven2 = weave_z(2)
+        woven3 = weave_z(3)
+        acc2 = cv_product(2, woven2)
+        acc3 = cv_product(3, woven3)
+        cv_gather(1, 0)
+        cv_gather(1, 1)
+        cv_out_of_psum(2, acc2)
+        finish(0, slice(0, N))
+        cv_out_of_psum(3, acc3)
+        cv_gather(2, 0)
+        cv_gather(2, 1)
+        finish(1, slice(0, N))
+        cv_gather(3, 0)
+        finish(2, slice(0, N))
+        cv_gather(3, 1)
+        finish(3, slice(0, HALF))
+        finish(3, slice(HALF, N))

@@ -19,7 +19,6 @@ AX = mybir.AxisListType
 P = 128
 PACK = 4
 PAD = 16
-RUNS = 8
 HALF = 256
 
 
@@ -41,42 +40,39 @@ def tile_picked_mombgsumglseover_none_p_kernel(
 
         table_scales = sb("table_scales", [P, T], U8)
         nc.vector.memset(table_scales[:].bitcast(I32), 0)
-        gi_cols = sb("gi_cols", [P, PACK], F32)
-        nc.gpsimd.dma_start(gi_cols[:], gi.rearrange("(p t) o -> p (t o)", t=PACK))
-        gt_cols = sb("gt_cols", [P, PACK], F32)
-        nc.gpsimd.dma_start(gt_cols[:], gt.rearrange("(p t) o -> p (t o)", t=PACK))
 
-        two_l = load_list("two_l", two)
-        n2_l = load_list("n2_l", n2)
-        table_words = sb("table_words", [P, T], I32)
-        nc.sync.dma_start(table_words[:], x_words[0].rearrange("p c r -> p (c r)").bitcast(I32))
+        offs_l = load_list("offs_l", offs)
+        n1_l = load_list("n1_l", n1)
+        gt_cols = sb("gt_cols", [P, PACK], F32)
+        nc.sync.dma_start(gt_cols[:], gt.rearrange("(p t) o -> p (t o)", t=PACK))
         for q in range(4):
             nc.sync.dma_start(
                 table_scales[32 * q : 32 * q + 4, :].bitcast(I32),
                 x_scales[0, 4 * q : 4 * q + 4, :].bitcast(I32),
             )
-        wb_rows = wb.rearrange("(p j) n -> p j n", j=PACK)
-        wb_raw = []
+        table_words = sb("table_words", [P, T], I32)
+        nc.sync.dma_start(table_words[:], x_words[0].rearrange("p c r -> p (c r)").bitcast(I32))
+        wa_rows = wa.rearrange("(p j) n -> p j n", j=PACK)
+        wa_raw = []
         for u in range(2):
-            raw = sb("wb_raw%d" % u, [P, PACK, HALF], F32)
-            nc.sync.dma_start(raw[:], wb_rows[:, :, u * HALF : (u + 1) * HALF])
-            wb_raw.append(raw)
-        wa_raw = sb("wa_raw", [P, PACK, H], F32)
-        nc.sync.dma_start(wa_raw[:], wa.rearrange("(p j) n -> p j n", j=PACK))
-        offs_l = load_list("offs_l", offs)
+            raw = sb("wa_raw%d" % u, [P, PACK, HALF], F32)
+            nc.sync.dma_start(raw[:], wa_rows[:, :, u * HALF : (u + 1) * HALF])
+            wa_raw.append(raw)
+        wb_raw = sb("wb_raw", [P, PACK, N], F32)
+        nc.sync.dma_start(wb_raw[:], wb.rearrange("(p j) n -> p j n", j=PACK))
+        two_l = load_list("two_l", two)
+        n2_l = load_list("n2_l", n2)
         n3_l = load_list("n3_l", n3)
-        n1_l = load_list("n1_l", n1)
+        gi_cols = sb("gi_cols", [P, PACK], F32)
+        nc.sync.dma_start(gi_cols[:], gi.rearrange("(p t) o -> p (t o)", t=PACK))
         n4_l = load_list("n4_l", n4)
         n5_l = load_list("n5_l", n5)
 
-        def window(name):
-            tile = sb(name, [P, N + PAD], F32)
-            nc.gpsimd.memset(tile[:, N:], 0.0)
+        def window(name, width, tag=None):
+            tile = sb(name, [P, width], F32, tag=tag)
+            nc.vector.memset(tile[:, N:], 0.0)
             return tile
 
-        ex_win = [window("ex_win%d" % t) for t in range(PACK)]
-        gb_win = [window("gb_win%d" % t) for t in range(PACK)]
-        a_win = [window("a_win%d" % t) for t in range(PACK)]
 
         def pick_words(name, lst):
             words = sb(name, [P, S], U32)
@@ -111,220 +107,223 @@ def tile_picked_mombgsumglseover_none_p_kernel(
                 rhs=rhs.bitcast(FP8X4), rhs_scale=rhs_scale, start=True, stop=True,
             )
 
-        xb_words = pick_words("xb_words", two_l)
-        xb_scales = pick_scales("xb_scales", two_l)
-        wb_codes = sb("wb_codes", [P, N], U32)
-        wb_scales = sb("wb_scales", [P, N], U8)
-        wb_woven = []
-        for u in range(2):
-            woven = sb("wb_woven%d" % u, [P, PACK * HALF], BF16)
-            dst, src = weave_views(woven[:], wb_raw[u][:])
-            if u == 0:
-                nc.scalar.copy(dst, src)
-            else:
-                nc.vector.tensor_copy(dst, src)
-            wb_woven.append(woven)
-        for u in range(2):
-            cols = slice(u * HALF, (u + 1) * HALF)
-            nc.vector.quantize_mx(wb_codes[:, cols].bitcast(FP8X4), wb_scales[:, cols], wb_woven[u][:])
-        b_acc = []
-        for t in range(PACK):
-            acc = psum.tile([P, N], F32, name="b_acc%d" % t, tag="bank%d" % t)
-            rows = slice(t * P, (t + 1) * P)
-            for u in range(2):
-                cols = slice(u * HALF, (u + 1) * HALF)
-                mx_pass(acc[:, cols], xb_words[:, rows], xb_scales[:, rows], wb_codes[:, cols], wb_scales[:, cols])
-            b_acc.append(acc)
-
-        ex_sum = sb("ex_sum", [P, PACK, N], F32)
-        ex_n2 = [sb("ex_n2_%d" % t, [P, N], F32) for t in range(PACK)]
-
-        def exp_step(t):
-            nc.scalar.activation(ex_win[t][:, :N], b_acc[t][:], ACT.Exp)
-            gather(ex_n2[t][:], ex_win[t][:], n2_l[:])
-            nc.vector.tensor_scalar(gb_win[t][:, :N], b_acc[t][:], gi_cols[:, t : t + 1], None, ALU.mult)
-
-        def add_step(t):
-            nc.vector.tensor_tensor(ex_sum[:, t, :], ex_win[t][:, :N], ex_n2[t][:], ALU.add)
-
-        exp_step(0)
-        xa_words = pick_words("xa_words", offs_l)
-        add_step(0)
-        exp_step(1)
         xa_scales = pick_scales("xa_scales", offs_l)
-        add_step(1)
-        exp_step(2)
-        wa_woven = sb("wa_woven", [P, PACK * H], BF16)
-        dst, src = weave_views(wa_woven[:], wa_raw[:])
-        nc.vector.tensor_copy(dst, src)
-        add_step(2)
-        exp_step(3)
+        xa_words = pick_words("xa_words", offs_l)
+        a_win = [window("a_win%d" % t, 2 * H + PAD) for t in range(PACK)]
+        ex_win = [window("ex_win%d" % t, N + PAD) for t in range(PACK)]
+        gb_win = [window("gb_win%d" % t, N + PAD) for t in range(PACK)]
         wa_codes = sb("wa_codes", [P, H], U32)
         wa_scales = sb("wa_scales", [P, H], U8)
-        nc.vector.quantize_mx(wa_codes[:].bitcast(FP8X4), wa_scales[:], wa_woven[:])
-        add_step(3)
-
-        gb_n3 = [sb("gb_n3_%d" % t, [P, N], F32) for t in range(PACK)]
-        for t in range(PACK):
-            gather(gb_n3[t][:], gb_win[t][:], n3_l[:])
-        lse = sb("lse", [P, PACK, N], F32)
-        nc.scalar.activation(lse[:], ex_sum[:], ACT.Ln)
-
-        for t in range(PACK):
+        parts = ((0, 0, HALF, nc.vector.tensor_copy), (1, 0, P, nc.vector.tensor_copy), (1, P, HALF, nc.scalar.copy))
+        for i, (u, c0, c1, copy) in enumerate(parts):
+            woven = sb("wa_woven%d" % i, [P, PACK * (c1 - c0)], BF16)
+            dst, src = weave_views(woven[:], wa_raw[u][:, :, c0:c1])
+            copy(dst, src)
+            cols = slice(u * HALF + c0, u * HALF + c1)
+            nc.vector.quantize_mx(wa_codes[:, cols].bitcast(FP8X4), wa_scales[:, cols], woven[:])
+        for i, (u, c0, c1, copy) in enumerate(parts):
+            cols = slice(u * HALF + c0, u * HALF + c1)
+            acc = psum.tile([P, c1 - c0], F32, name="a_first%d" % i, tag="bank%d" % i)
+            mx_pass(acc[:], xa_words[:, :P], xa_scales[:, :P], wa_codes[:, cols], wa_scales[:, cols])
+            (nc.scalar.copy if i == 0 else nc.vector.tensor_copy)(a_win[0][:, cols], acc[:])
+        for t in range(1, PACK):
             acc = psum.tile([P, H], F32, name="a_acc%d" % t, tag="bank%d" % (PACK + t))
             rows = slice(t * P, (t + 1) * P)
             mx_pass(acc[:], xa_words[:, rows], xa_scales[:, rows], wa_codes[:], wa_scales[:])
             nc.vector.tensor_copy(a_win[t][:, :H], acc[:])
+        half_gt = sb("half_gt", [P, PACK], F32)
+        nc.vector.tensor_scalar(half_gt[:], gt_cols[:], 0.5, None, ALU.mult)
 
-        z2_rows = sb("z2_rows", [P, PACK, N], BF16)
-        for t in range(PACK):
-            nc.vector.scalar_tensor_tensor(
-                z2_rows[:, t, :], lse[:, t, :], gi_cols[:, t : t + 1], gb_n3[t][:], ALU.mult, ALU.subtract
-            )
-        z2_woven = sb("z2_woven", [P, PACK * N], BF16)
-        dst, src = weave_views(z2_woven[:], z2_rows[:])
-        nc.vector.tensor_copy(dst, src)
-        z2_codes = sb("z2_codes", [P, N], U32)
-        z2_scales = sb("z2_scales", [P, N], U8)
-        nc.vector.quantize_mx(z2_codes[:].bitcast(FP8X4), z2_scales[:], z2_woven[:])
+        z_rows = sb("z_rows", [P, PACK, H], BF16)
 
-        z_rows = [sb("z_rows%d" % u, [P, PACK, HALF], BF16) for u in range(2)]
-
-        def sum4(dst, src):
-            nc.vector.tensor_reduce(dst, src.rearrange("p (j f) -> p j f", f=4), AX.X, ALU.add)
-
-        def z_step(t, u, sig):
-            nc.vector.scalar_tensor_tensor(
-                z_rows[u][:, t, :].rearrange("p (r k) -> p r k", r=RUNS),
-                a_win[t][:, :H].rearrange("p (r u k) -> p r u k", r=RUNS, u=2)[:, :, u, :],
-                gt_cols[:, t : t + 1], sig, ALU.mult, ALU.mult,
-            )
-
-        def whole_gather(t):
+        def n1_gather(t):
             mb = sb("mb%d" % t, [P, W], F32)
-            for q in range(4):
-                gather(mb[:, q * 512 : (q + 1) * 512], a_win[t][:], n1_l[:, q * 32 : (q + 1) * 32])
+            for q in range(2):
+                gather(mb[:, q * 1024 : (q + 1) * 1024], a_win[t][:], n1_l[:, q * 64 : (q + 1) * 64])
             return mb
 
-        def whole_sums(t, mb):
+        def sums(t, mb):
             ms = sb("ms%d" % t, [P, H], F32, tag="hold%d" % t)
             for q in range(2):
-                sum4(ms[:, q * HALF : (q + 1) * HALF], mb[:, q * 1024 : (q + 1) * 1024])
-            sig = sb("sig%d" % t, [P, H], F32)
-            nc.scalar.activation(sig[:], ms[:], ACT.Sigmoid)
-            return sig[:].rearrange("p (r u k) -> p r u k", r=RUNS, u=2)
+                nc.vector.tensor_reduce(
+                    ms[:, q * HALF : (q + 1) * HALF],
+                    mb[:, q * 1024 : (q + 1) * 1024].rearrange("p (j f) -> p j f", f=4), AX.X, ALU.add,
+                )
+            return ms
 
-        def part_gather(t, u, r0, r1, tag=None):
-            mb = sb("mb%d_%d_%d" % (t, u, r0), [P, (r1 - r0) * 128], F32, tag=tag)
-            for r in range(r0, r1):
-                c0 = 16 * r + 8 * u
-                gather(mb[:, (r - r0) * 128 : (r - r0 + 1) * 128], a_win[t][:], n1_l[:, c0 : c0 + 8])
-            return mb
+        def tanh_step(t, ms):
+            th = sb("th%d" % t, [P, H], F32)
+            nc.scalar.activation(th[:], ms[:], ACT.Tanh, scale=0.5)
+            return th
 
-        def half_ms(t, u):
-            return sb("ms%d_%d" % (t, u), [P, HALF], F32, tag="hold%d_%d" % (t, u))
+        def z_step(t, th):
+            gate = sb("gate%d" % t, [P, H], F32)
+            col = half_gt[:, t : t + 1]
+            nc.vector.tensor_scalar(gate[:], th[:], col, col, ALU.mult, ALU.add)
+            nc.vector.tensor_tensor(z_rows[:, t, :], a_win[t][:, :H], gate[:], ALU.mult)
 
-        def half_sig(t, u, ms):
-            sig = sb("sig%d_%d" % (t, u), [P, HALF], F32)
-            nc.scalar.activation(sig[:], ms[:], ACT.Sigmoid)
-            return sig[:].rearrange("p (r k) -> p r k", r=RUNS)
+        mb0 = n1_gather(0)
+        mb1 = n1_gather(1)
+        th0 = tanh_step(0, sums(0, mb0))
+        mb2 = n1_gather(2)
+        xb_words = pick_words("xb_words", two_l)
+        xb_scales = pick_scales("xb_scales", two_l)
+        th1 = tanh_step(1, sums(1, mb1))
+        mb3 = n1_gather(3)
+        wb_woven = sb("wb_woven", [P, PACK * N], BF16)
+        dst, src = weave_views(wb_woven[:], wb_raw[:])
+        nc.vector.tensor_copy(dst, src)
+        z_step(0, th0)
+        wb_codes = sb("wb_codes", [P, N], U32)
+        wb_scales = sb("wb_scales", [P, N], U8)
+        nc.vector.quantize_mx(wb_codes[:].bitcast(FP8X4), wb_scales[:], wb_woven[:])
+        b_acc = []
+        for t in range(PACK):
+            acc = psum.tile([P, N], F32, name="b_acc%d" % t, tag="bank%d" % t)
+            rows = slice(t * P, (t + 1) * P)
+            mx_pass(acc[:], xb_words[:, rows], xb_scales[:, rows], wb_codes[:], wb_scales[:])
+            b_acc.append(acc)
+        th2 = tanh_step(2, sums(2, mb2))
+        cv_win = [window("cv_win%d" % c, 2 * N, tag=old) for c, old in enumerate(("mb0", "mb1", "wb_raw", "hold0"))]
+        th3 = tanh_step(3, sums(3, mb3))
 
-        cv_win = [sb("cv_win%d" % c, [P, N], F32) for c in range(4)]
+        ex_sum = sb("ex_sum", [P, PACK, N], F32)
+        ex_n2 = sb("ex_n2", [P, PACK, N], F32, tag="hold3")
 
-        def weave_z(c):
-            u, e = divmod(c, 2)
-            woven = sb("z_woven%d" % c, [P, PACK * P], BF16)
-            nc.vector.tensor_copy(
-                woven[:].rearrange("p (r a i t) -> p r a t i", r=RUNS, a=4, i=4),
-                z_rows[u][:].rearrange("p t (r e a i) -> p e r a t i", r=RUNS, e=2, a=4)[:, e],
+        def gb_step(t):
+            nc.vector.tensor_scalar(gb_win[t][:, :N], b_acc[t][:], gi_cols[:, t : t + 1], None, ALU.mult)
+
+        def add_step(t):
+            nc.vector.tensor_tensor(ex_sum[:, t, :], ex_win[t][:, :N], ex_n2[:, t, :], ALU.add)
+
+        for t in range(PACK):
+            nc.scalar.activation(ex_win[t][:, :N], b_acc[t][:], ACT.Exp)
+        for t in range(PACK):
+            gather(ex_n2[:, t, :], ex_win[t][:], n2_l[:])
+        gb_step(0)
+        z_step(1, th1)
+        z_step(2, th2)
+        z_step(3, th3)
+        gb_step(1)
+        add_step(0)
+        gb_step(2)
+        z_woven = sb("z_woven", [P, PACK * H], BF16)
+        nc.vector.tensor_copy(
+            z_woven[:].rearrange("p (c m t) -> p c m t", c=PACK, t=PACK),
+            z_rows[:].rearrange("p t (m c) -> p c m t", c=PACK),
+        )
+        gb_step(3)
+        add_step(1)
+        z_codes = sb("z_codes", [P, H], U32)
+        z_scales = sb("z_scales", [P, H], U8)
+        nc.vector.quantize_mx(z_codes[:].bitcast(FP8X4), z_scales[:], z_woven[:])
+        add_step(2)
+        add_step(3)
+
+        chunks = (slice(0, 256), slice(256, 384), slice(384, 512))
+        gb_n3 = {}
+
+        def n3_gather(k, t, dst):
+            cols = chunks[k]
+            gather(dst, gb_win[t][:], n3_l[:, cols.start // 16 : cols.stop // 16])
+            gb_n3[(k, t)] = dst
+
+        gb_first = sb("gb_first", [P, PACK, HALF], F32)
+        for t in range(PACK):
+            n3_gather(0, t, gb_first[:, t, :])
+
+        lse = sb("lse", [P, PACK, N], F32)
+        for t in range(PACK):
+            nc.scalar.activation(lse[:, t, :HALF], ex_sum[:, t, :HALF], ACT.Ln)
+        nc.scalar.activation(lse[:, :, HALF:], ex_sum[:, :, HALF:], ACT.Ln)
+
+        z2_rows = [sb("z2_rows%d" % k, [P, PACK, c.stop - c.start], BF16) for k, c in enumerate(chunks[:2])]
+        z2_woven = [sb("z2_woven%d" % k, [P, PACK * (c.stop - c.start)], BF16) for k, c in enumerate(chunks)]
+        z2_codes = sb("z2_codes", [P, N], U32)
+        z2_scales = sb("z2_scales", [P, N], U8)
+        first_lo = psum.tile([P, N], F32, name="first_lo", tag="bank0")
+        first_hi = psum.tile([P, N], F32, name="first_hi", tag="bank4")
+
+        def z2_step(k, t):
+            if k == 2:
+                dst = z2_woven[k][:].rearrange("p (j t) -> p t j", t=PACK)[:, t, :]
+            else:
+                dst = z2_rows[k][:, t, :]
+            nc.vector.scalar_tensor_tensor(
+                dst, lse[:, t, chunks[k]], gi_cols[:, t : t + 1], gb_n3[(k, t)],
+                ALU.mult, ALU.subtract,
             )
-            return woven
 
-        def cv_product(c, woven):
-            codes = sb("z_codes%d" % c, [P, P], U32)
-            scales = sb("z_scales%d" % c, [P, P], U8)
-            nc.vector.quantize_mx(codes[:].bitcast(FP8X4), scales[:], woven[:])
+        def z2_weave(k):
+            dst, src = weave_views(z2_woven[k][:], z2_rows[k][:])
+            nc.vector.tensor_copy(dst, src)
+
+        def cv_products(k):
+            cols = chunks[k]
+            nc.vector.quantize_mx(z2_codes[:, cols].bitcast(FP8X4), z2_scales[:, cols], z2_woven[k][:])
+            acc = first_hi if k == 2 else first_lo
+            mx_pass(acc[:, cols], z_codes[:, :P], z_scales[:, :P], z2_codes[:, cols], z2_scales[:, cols])
+
+        lo, hi = slice(0, 384), slice(384, N)
+
+        def cv_rest(c):
+            rows = slice(c * P, (c + 1) * P)
             acc = psum.tile([P, N], F32, name="cv_acc%d" % c, tag="bank%d" % c)
-            mx_pass(acc[:], codes[:], scales[:], z2_codes[:], z2_scales[:])
-            return acc
+            mx_pass(acc[:], z_codes[:, rows], z_scales[:, rows], z2_codes[:], z2_scales[:])
+            nc.vector.tensor_scalar(cv_win[c][:, :N], acc[:], 0.0625, None, ALU.mult)
 
-        def cv_out_of_psum(c, acc):
-            nc.vector.tensor_scalar(cv_win[c][:], acc[:], 0.0625, None, ALU.mult)
+        for t in range(PACK):
+            z2_step(0, t)
+        for t in range(PACK):
+            n3_gather(1, t, ex_sum[:, t, chunks[1]])
+        z2_weave(0)
+        z2_step(1, 0)
+        cv_products(0)
+        for t in range(1, PACK):
+            z2_step(1, t)
+        for t in range(PACK):
+            n3_gather(2, t, ex_sum[:, t, chunks[2]])
+        z2_step(2, 0)
+        z2_weave(1)
+        z2_step(2, 1)
+        cv_products(1)
+        z2_step(2, 2)
+        z2_step(2, 3)
+        nc.scalar.activation(cv_win[0][:, lo], first_lo[:, lo], ACT.Copy, scale=0.0625)
+        cv_products(2)
+        nc.vector.tensor_scalar(cv_win[0][:, hi], first_hi[:, hi], 0.0625, None, ALU.mult)
+        for c in range(1, PACK):
+            cv_rest(c)
 
-        g4 = [sb("g4_%d" % c, [P, N], F32) for c in range(4)]
-        g5 = [sb("g5_%d" % c, [P, N], F32) for c in range(4)]
-        top = [sb("top%d" % c, [P, N], F32) for c in range(4)]
-        res = [sb("res%d" % c, [P, N], F32) for c in range(4)]
-        out_rows = out.rearrange("(r c i) n -> c r i n", r=RUNS, c=4)
+        g4 = [sb("g4_%d" % c, [P, N], F32) for c in range(PACK)]
+        g5 = [sb("g5_%d" % c, [P, N], F32) for c in range(PACK)]
+        top = {}
+        res = [sb("res%d" % c, [P, N], F32) for c in range(PACK)]
+        out_rows = out.rearrange("(p c) n -> c p n", c=PACK)
 
-        def cv_gather(c, v):
-            cols = slice(v * HALF, (v + 1) * HALF)
-            gather(g4[c][:, cols], cv_win[c][:], n4_l[:, 16 * v : 16 * v + 16])
-            gather(g5[c][:, cols], cv_win[c][:], n5_l[:, 16 * v : 16 * v + 16])
+        def cv_gather(c, cols):
+            lst = slice(cols.start // 16, cols.stop // 16)
+            gather(g4[c][:, cols], cv_win[c][:], n4_l[:, lst])
+            gather(g5[c][:, cols], cv_win[c][:], n5_l[:, lst])
 
         def finish(c, cols):
+            if c not in top:
+                top[c] = sb("top%d" % c, [P, N], F32, tag="top")
             nc.vector.tensor_tensor(top[c][:, cols], g4[c][:, cols], g5[c][:, cols], ALU.max)
             nc.vector.scalar_tensor_tensor(
                 res[c][:, cols], cv_win[c][:, cols], -0.75, top[c][:, cols], ALU.mult, ALU.add
             )
-            nc.sync.dma_start(out_rows[c][:, :, cols], res[c][:, cols])
+            nc.sync.dma_start(out_rows[c][:, cols], res[c][:, cols])
 
-        mb0 = whole_gather(0)
-        mb1 = whole_gather(1)
-        sig0 = whole_sums(0, mb0)
-        mb20 = part_gather(2, 0, 0, 8, tag="hold0")
-        sig1 = whole_sums(1, mb1)
-        z_step(0, 0, sig0[:, :, 0, :])
-        mb30a = part_gather(3, 0, 0, 6, tag="hold1")
-        mb30b = part_gather(3, 0, 6, 8)
-        ms20 = half_ms(2, 0)
-        sum4(ms20[:], mb20[:])
-        sig20 = half_sig(2, 0, ms20)
-        z_step(1, 0, sig1[:, :, 0, :])
-        z_step(0, 1, sig0[:, :, 1, :])
-        z_step(1, 1, sig1[:, :, 1, :])
-        ms30 = half_ms(3, 0)
-        sum4(ms30[:, :192], mb30a[:])
-        z_step(2, 0, sig20)
-        mb21a = part_gather(2, 1, 0, 2, tag="hold2_0")
-        sum4(ms30[:, 192:], mb30b[:])
-        sig30 = half_sig(3, 0, ms30)
-        mb21b = part_gather(2, 1, 2, 8, tag="hold3_0")
-        z_step(3, 0, sig30)
-        woven0 = weave_z(0)
-        woven1 = weave_z(1)
-        acc0 = cv_product(0, woven0)
-        acc1 = cv_product(1, woven1)
-        ms21 = half_ms(2, 1)
-        sum4(ms21[:, :64], mb21a[:])
-        sum4(ms21[:, 64:], mb21b[:])
-        mb31a = part_gather(3, 1, 0, 4)
-        sig21 = half_sig(2, 1, ms21)
-        mb31b = part_gather(3, 1, 4, 8, tag="hold2_1")
-        cv_out_of_psum(0, acc0)
-        ms31 = half_ms(3, 1)
-        sum4(ms31[:, :128], mb31a[:])
-        z_step(2, 1, sig21)
-        cv_gather(0, 0)
-        sum4(ms31[:, 128:], mb31b[:])
-        sig31 = half_sig(3, 1, ms31)
-        cv_out_of_psum(1, acc1)
-        cv_gather(0, 1)
-        z_step(3, 1, sig31)
-        woven2 = weave_z(2)
-        woven3 = weave_z(3)
-        acc2 = cv_product(2, woven2)
-        acc3 = cv_product(3, woven3)
-        cv_gather(1, 0)
-        cv_gather(1, 1)
-        cv_out_of_psum(2, acc2)
-        finish(0, slice(0, N))
-        cv_out_of_psum(3, acc3)
-        cv_gather(2, 0)
-        cv_gather(2, 1)
-        finish(1, slice(0, N))
-        cv_gather(3, 0)
-        finish(2, slice(0, N))
-        cv_gather(3, 1)
+        whole = slice(0, N)
+        cv_gather(0, whole)
+        cv_gather(1, whole)
+        finish(0, whole)
+        cv_gather(2, whole)
+        finish(1, whole)
+        gather(g4[3][:], cv_win[3][:], n4_l[:])
+        finish(2, whole)
+        gather(g5[3][:, :HALF], cv_win[3][:], n5_l[:, :16])
+        gather(g5[3][:, HALF:], cv_win[3][:], n5_l[:, 16:])
         finish(3, slice(0, HALF))
         finish(3, slice(HALF, N))

@@ -68,22 +68,22 @@ def tile_picked_mombgsumglseover_none_p_kernel(
         n4_l = load_list("n4_l", n4)
         n5_l = load_list("n5_l", n5)
 
-        def window(name, width, tag=None):
+        def window(name, width, tag=None, engine=nc.vector):
             tile = sb(name, [P, width], F32, tag=tag)
-            nc.vector.memset(tile[:, N:], 0.0)
+            engine.memset(tile[:, N:], 0.0)
             return tile
 
 
-        def pick_words(name, lst):
-            words = sb(name, [P, S], U32)
+        def pick_words(name, lst, tag=None):
+            words = sb(name, [P, S], U32, tag=tag)
             nc.vector.tensor_copy(
                 words[:].rearrange("p (t m) -> p m t", t=PACK),
                 table_words[:].bitcast(U32).indirect(lst[:]),
             )
             return words
 
-        def pick_scales(name, lst):
-            picked = sb(name + "_listed", [P, S], U8)
+        def pick_scales(name, lst, tag=None):
+            picked = sb(name + "_listed", [P, S], U8, tag=tag)
             nc.vector.tensor_copy(picked[:], table_scales[:].indirect(lst[:]))
             dealt = sb(name, [P, S], U8)
             nc.vector.tensor_copy(
@@ -109,8 +109,11 @@ def tile_picked_mombgsumglseover_none_p_kernel(
 
         xa_scales = pick_scales("xa_scales", offs_l)
         xa_words = pick_words("xa_words", offs_l)
-        a_win = [window("a_win%d" % t, 2 * H + PAD) for t in range(PACK)]
-        ex_win = [window("ex_win%d" % t, N + PAD) for t in range(PACK)]
+        a_win = [
+            window("a_win%d" % t, (W if t < PACK - 1 else W // 2) + PAD, engine=nc.gpsimd if t in (1, 2) else nc.vector)
+            for t in range(PACK)
+        ]
+        ex_win = [window("ex_win%d" % t, N + PAD) for t in range(PACK - 1)]
         gb_win = [window("gb_win%d" % t, N + PAD) for t in range(PACK)]
         wa_codes = sb("wa_codes", [P, H], U32)
         wa_scales = sb("wa_scales", [P, H], U8)
@@ -138,8 +141,9 @@ def tile_picked_mombgsumglseover_none_p_kernel(
 
         def n1_gather(t):
             mb = sb("mb%d" % t, [P, W], F32)
-            for q in range(2):
-                gather(mb[:, q * 1024 : (q + 1) * 1024], a_win[t][:], n1_l[:, q * 64 : (q + 1) * 64])
+            step = W if t < PACK - 1 else W // 2
+            for q in range(0, W, step):
+                gather(mb[:, q : q + step], a_win[t][:], n1_l[:, q // 16 : (q + step) // 16])
             return mb
 
         def sums(t, mb):
@@ -166,14 +170,13 @@ def tile_picked_mombgsumglseover_none_p_kernel(
         mb1 = n1_gather(1)
         th0 = tanh_step(0, sums(0, mb0))
         mb2 = n1_gather(2)
-        xb_words = pick_words("xb_words", two_l)
-        xb_scales = pick_scales("xb_scales", two_l)
+        xb_words = pick_words("xb_words", two_l, tag="wa_codes")
+        xb_scales = pick_scales("xb_scales", two_l, tag="wa_scales")
         th1 = tanh_step(1, sums(1, mb1))
         mb3 = n1_gather(3)
-        wb_woven = sb("wb_woven", [P, PACK * N], BF16)
+        wb_woven = sb("wb_woven", [P, PACK * N], BF16, tag="xa_words")
         dst, src = weave_views(wb_woven[:], wb_raw[:])
         nc.vector.tensor_copy(dst, src)
-        z_step(0, th0)
         wb_codes = sb("wb_codes", [P, N], U32)
         wb_scales = sb("wb_scales", [P, N], U8)
         nc.vector.quantize_mx(wb_codes[:].bitcast(FP8X4), wb_scales[:], wb_woven[:])
@@ -183,42 +186,48 @@ def tile_picked_mombgsumglseover_none_p_kernel(
             rows = slice(t * P, (t + 1) * P)
             mx_pass(acc[:], xb_words[:, rows], xb_scales[:, rows], wb_codes[:], wb_scales[:])
             b_acc.append(acc)
+        cv_win = [window("cv_win%d" % c, 2 * N, tag=old) for c, old in enumerate(("mb0", "mb1", "wb_raw", "xa_words"))]
         th2 = tanh_step(2, sums(2, mb2))
-        cv_win = [window("cv_win%d" % c, 2 * N, tag=old) for c, old in enumerate(("mb0", "mb1", "wb_raw", "hold0"))]
+        z_step(0, th0)
         th3 = tanh_step(3, sums(3, mb3))
+        ex_win.append(window("ex_win3", N + PAD, tag="mb3"))
 
-        ex_sum = sb("ex_sum", [P, PACK, N], F32)
+        ex_sum = sb("ex_sum", [P, N // P, PACK, P], F32)
         ex_n2 = sb("ex_n2", [P, PACK, N], F32, tag="hold3")
+
+        def by_quarter(ap):
+            return ap.rearrange("p (q j) -> p q j", j=P)
 
         def gb_step(t):
             nc.vector.tensor_scalar(gb_win[t][:, :N], b_acc[t][:], gi_cols[:, t : t + 1], None, ALU.mult)
 
         def add_step(t):
-            nc.vector.tensor_tensor(ex_sum[:, t, :], ex_win[t][:, :N], ex_n2[:, t, :], ALU.add)
+            nc.vector.tensor_tensor(
+                ex_sum[:, :, t, :], by_quarter(ex_win[t][:, :N]), by_quarter(ex_n2[:, t, :]), ALU.add
+            )
 
         for t in range(PACK):
             nc.scalar.activation(ex_win[t][:, :N], b_acc[t][:], ACT.Exp)
         for t in range(PACK):
             gather(ex_n2[:, t, :], ex_win[t][:], n2_l[:])
         gb_step(0)
-        z_step(1, th1)
-        z_step(2, th2)
-        z_step(3, th3)
         gb_step(1)
-        add_step(0)
+        for t, th in ((1, th1), (2, th2), (3, th3)):
+            z_step(t, th)
         gb_step(2)
+        gb_step(3)
+        add_step(0)
+        add_step(1)
         z_woven = sb("z_woven", [P, PACK * H], BF16)
         nc.vector.tensor_copy(
             z_woven[:].rearrange("p (c m t) -> p c m t", c=PACK, t=PACK),
             z_rows[:].rearrange("p t (m c) -> p c m t", c=PACK),
         )
-        gb_step(3)
-        add_step(1)
+        add_step(2)
+        add_step(3)
         z_codes = sb("z_codes", [P, H], U32)
         z_scales = sb("z_scales", [P, H], U8)
         nc.vector.quantize_mx(z_codes[:].bitcast(FP8X4), z_scales[:], z_woven[:])
-        add_step(2)
-        add_step(3)
 
         chunks = (slice(0, 256), slice(256, 384), slice(384, 512))
         gb_n3 = {}
@@ -228,43 +237,46 @@ def tile_picked_mombgsumglseover_none_p_kernel(
             gather(dst, gb_win[t][:], n3_l[:, cols.start // 16 : cols.stop // 16])
             gb_n3[(k, t)] = dst
 
-        gb_first = sb("gb_first", [P, PACK, HALF], F32)
+        gb_early = sb("gb_early", [P, PACK, HALF], F32)
         for t in range(PACK):
-            n3_gather(0, t, gb_first[:, t, :])
+            n3_gather(0, t, gb_early[:, t, :])
 
-        lse = sb("lse", [P, PACK, N], F32)
+        lse_lo = sb("lse_lo", [P, PACK, HALF], F32)
+        lse_hi = sb("lse_hi", [P, 2, PACK, P], F32)
         for t in range(PACK):
-            nc.scalar.activation(lse[:, t, :HALF], ex_sum[:, t, :HALF], ACT.Ln)
-        nc.scalar.activation(lse[:, :, HALF:], ex_sum[:, :, HALF:], ACT.Ln)
+            nc.scalar.activation(by_quarter(lse_lo[:, t, :]), ex_sum[:, :2, t, :], ACT.Ln)
+        nc.scalar.activation(lse_hi[:], ex_sum[:, 2:], ACT.Ln)
 
-        z2_rows = [sb("z2_rows%d" % k, [P, PACK, c.stop - c.start], BF16) for k, c in enumerate(chunks[:2])]
+        z2_rows = [sb("z2_rows%d" % k, [P, PACK, c.stop - c.start], BF16) for k, c in enumerate(chunks)]
         z2_woven = [sb("z2_woven%d" % k, [P, PACK * (c.stop - c.start)], BF16) for k, c in enumerate(chunks)]
         z2_codes = sb("z2_codes", [P, N], U32)
         z2_scales = sb("z2_scales", [P, N], U8)
-        first_lo = psum.tile([P, N], F32, name="first_lo", tag="bank0")
-        first_hi = psum.tile([P, N], F32, name="first_hi", tag="bank4")
+        first_acc = [
+            psum.tile([P, c.stop - c.start], F32, name="first_acc%d" % k, tag="bank%d" % (PACK + k))
+            for k, c in enumerate(chunks)
+        ]
 
-        def z2_step(k, t):
-            if k == 2:
+        def z2_step(k, t, direct=False):
+            cols = chunks[k]
+            dst, looked_up = z2_rows[k][:, t, :], gb_n3[(k, t)]
+            if direct:
                 dst = z2_woven[k][:].rearrange("p (j t) -> p t j", t=PACK)[:, t, :]
+            if k == 0:
+                log_sum = lse_lo[:, t, :]
+            elif cols.stop - cols.start == P:
+                log_sum = lse_hi[:, cols.start // P - 2, t, :]
             else:
-                dst = z2_rows[k][:, t, :]
-            nc.vector.scalar_tensor_tensor(
-                dst, lse[:, t, chunks[k]], gi_cols[:, t : t + 1], gb_n3[(k, t)],
-                ALU.mult, ALU.subtract,
-            )
+                log_sum, dst, looked_up = lse_hi[:, :, t, :], by_quarter(dst), by_quarter(looked_up)
+            nc.vector.scalar_tensor_tensor(dst, log_sum, gi_cols[:, t : t + 1], looked_up, ALU.mult, ALU.subtract)
 
-        def z2_weave(k):
+        def z2_weave(k, rows=PACK):
             dst, src = weave_views(z2_woven[k][:], z2_rows[k][:])
-            nc.vector.tensor_copy(dst, src)
+            nc.vector.tensor_copy(dst[:, :, :rows, :], src[:, :, :rows, :])
 
         def cv_products(k):
             cols = chunks[k]
             nc.vector.quantize_mx(z2_codes[:, cols].bitcast(FP8X4), z2_scales[:, cols], z2_woven[k][:])
-            acc = first_hi if k == 2 else first_lo
-            mx_pass(acc[:, cols], z_codes[:, :P], z_scales[:, :P], z2_codes[:, cols], z2_scales[:, cols])
-
-        lo, hi = slice(0, 384), slice(384, N)
+            mx_pass(first_acc[k][:], z_codes[:, :P], z_scales[:, :P], z2_codes[:, cols], z2_scales[:, cols])
 
         def cv_rest(c):
             rows = slice(c * P, (c + 1) * P)
@@ -272,26 +284,26 @@ def tile_picked_mombgsumglseover_none_p_kernel(
             mx_pass(acc[:], z_codes[:, rows], z_scales[:, rows], z2_codes[:], z2_scales[:])
             nc.vector.tensor_scalar(cv_win[c][:, :N], acc[:], 0.0625, None, ALU.mult)
 
+        spent = ex_sum[:].rearrange("p q t j -> p (q t j)")
         for t in range(PACK):
             z2_step(0, t)
-        for t in range(PACK):
-            n3_gather(1, t, ex_sum[:, t, chunks[1]])
         z2_weave(0)
-        z2_step(1, 0)
         cv_products(0)
-        for t in range(1, PACK):
-            z2_step(1, t)
+        for t, at in enumerate((3, 7, 8, 9)):
+            n3_gather(1, t, spent[:, at * P : at * P + 128])
         for t in range(PACK):
-            n3_gather(2, t, ex_sum[:, t, chunks[2]])
-        z2_step(2, 0)
+            z2_step(1, t)
         z2_weave(1)
-        z2_step(2, 1)
         cv_products(1)
-        z2_step(2, 2)
-        z2_step(2, 3)
-        nc.scalar.activation(cv_win[0][:, lo], first_lo[:, lo], ACT.Copy, scale=0.0625)
+        for t, at in enumerate((10, 11, 12, 13)):
+            n3_gather(2, t, spent[:, at * P : at * P + 128])
+        for t in range(PACK):
+            z2_step(2, t)
+        z2_weave(2)
         cv_products(2)
-        nc.vector.tensor_scalar(cv_win[0][:, hi], first_hi[:, hi], 0.0625, None, ALU.mult)
+        for k in range(2):
+            nc.scalar.activation(cv_win[0][:, chunks[k]], first_acc[k][:], ACT.Copy, scale=0.0625)
+        nc.vector.tensor_scalar(cv_win[0][:, chunks[2]], first_acc[2][:], 0.0625, None, ALU.mult)
         for c in range(1, PACK):
             cv_rest(c)
 

@@ -68,9 +68,9 @@ def tile_picked_mombgsumglseover_none_p_kernel(
         n4_l = load_list("n4_l", n4)
         n5_l = load_list("n5_l", n5)
 
-        def window(name, width, tag=None, engine=nc.vector):
+        def window(name, width, tag=None):
             tile = sb(name, [P, width], F32, tag=tag)
-            engine.memset(tile[:, N:], 0.0)
+            nc.vector.memset(tile[:, N:], 0.0)
             return tile
 
 
@@ -109,10 +109,7 @@ def tile_picked_mombgsumglseover_none_p_kernel(
 
         xa_scales = pick_scales("xa_scales", offs_l)
         xa_words = pick_words("xa_words", offs_l)
-        a_win = [
-            window("a_win%d" % t, (W if t < PACK - 1 else W // 2) + PAD, engine=nc.gpsimd if t in (1, 2) else nc.vector)
-            for t in range(PACK)
-        ]
+        a_win = [window("a_win%d" % t, 2 * H + PAD) for t in range(PACK)]
         ex_win = [window("ex_win%d" % t, N + PAD) for t in range(PACK - 1)]
         gb_win = [window("gb_win%d" % t, N + PAD) for t in range(PACK)]
         wa_codes = sb("wa_codes", [P, H], U32)
@@ -141,9 +138,8 @@ def tile_picked_mombgsumglseover_none_p_kernel(
 
         def n1_gather(t):
             mb = sb("mb%d" % t, [P, W], F32)
-            step = W if t < PACK - 1 else W // 2
-            for q in range(0, W, step):
-                gather(mb[:, q : q + step], a_win[t][:], n1_l[:, q // 16 : (q + step) // 16])
+            for q in range(2):
+                gather(mb[:, q * 1024 : (q + 1) * 1024], a_win[t][:], n1_l[:, q * 64 : (q + 1) * 64])
             return mb
 
         def sums(t, mb):

@@ -18,8 +18,15 @@ AX = mybir.AxisListType
 
 P = 128
 PACK = 4
+LAST = PACK - 1
+MEMBERS = W // H
+PER_COLUMN = 16
 PAD = 16
-HALF = 256
+HALF = N // 2
+LO, HI, WHOLE = slice(0, HALF), slice(HALF, N), slice(0, N)
+N1_CUTS = (0, W // 2, W)
+N1_CUTS_LAST = (0, W // 2, W - HALF, W)
+CHUNKS = (slice(0, HALF), slice(HALF, HALF + P), slice(HALF + P, N))
 
 
 def tile_picked_mombgsumglseover_none_p_kernel(
@@ -33,18 +40,28 @@ def tile_picked_mombgsumglseover_none_p_kernel(
         def sb(name, shape, dtype, tag=None):
             return held.tile(shape, dtype, name=name, tag=tag or name, align_bytes=64)
 
+        def bank(name, width, number):
+            return psum.tile([P, width], F32, name=name, tag="bank%d" % number)
+
         def load_list(name, src):
             tile = sb(name, list(src.shape), U16)
             nc.sync.dma_start(tile[:], src)
             return tile
 
+        def load_weights_of_places(name, src, tag=None):
+            tile = sb(name, [P, PACK], F32, tag=tag)
+            nc.sync.dma_start(tile[:], src.rearrange("(p t) o -> p (t o)", t=PACK))
+            return tile
+
+        def entries(lst, first, end):
+            return lst[:, first // PER_COLUMN : end // PER_COLUMN]
+
         table_scales = sb("table_scales", [P, T], U8)
         nc.vector.memset(table_scales[:].bitcast(I32), 0)
 
+        two_l = load_list("two_l", two)
+        n2_l = load_list("n2_l", n2)
         offs_l = load_list("offs_l", offs)
-        n1_l = load_list("n1_l", n1)
-        gt_cols = sb("gt_cols", [P, PACK], F32)
-        nc.sync.dma_start(gt_cols[:], gt.rearrange("(p t) o -> p (t o)", t=PACK))
         for q in range(4):
             nc.sync.dma_start(
                 table_scales[32 * q : 32 * q + 4, :].bitcast(I32),
@@ -52,27 +69,24 @@ def tile_picked_mombgsumglseover_none_p_kernel(
             )
         table_words = sb("table_words", [P, T], I32)
         nc.sync.dma_start(table_words[:], x_words[0].rearrange("p c r -> p (c r)").bitcast(I32))
-        wa_rows = wa.rearrange("(p j) n -> p j n", j=PACK)
-        wa_raw = []
-        for u in range(2):
-            raw = sb("wa_raw%d" % u, [P, PACK, HALF], F32)
-            nc.sync.dma_start(raw[:], wa_rows[:, :, u * HALF : (u + 1) * HALF])
-            wa_raw.append(raw)
-        wb_raw = sb("wb_raw", [P, PACK, N], F32)
-        nc.sync.dma_start(wb_raw[:], wb.rearrange("(p j) n -> p j n", j=PACK))
-        two_l = load_list("two_l", two)
-        n2_l = load_list("n2_l", n2)
+        wb_rows = wb.rearrange("(p j) n -> p j n", j=PACK)
+        wb_raw = []
+        for u, cols in enumerate((LO, HI)):
+            raw = sb("wb_raw%d" % u, [P, PACK, HALF], F32)
+            nc.sync.dma_start(raw[:], wb_rows[:, :, cols])
+            wb_raw.append(raw)
+        wa_raw = sb("wa_raw", [P, PACK, H], F32)
+        nc.sync.dma_start(wa_raw[:], wa.rearrange("(p j) n -> p j n", j=PACK))
+        n1_l = load_list("n1_l", n1)
+        gt_cols = load_weights_of_places("gt_cols", gt)
         n3_l = load_list("n3_l", n3)
-        gi_cols = sb("gi_cols", [P, PACK], F32)
-        nc.sync.dma_start(gi_cols[:], gi.rearrange("(p t) o -> p (t o)", t=PACK))
         n4_l = load_list("n4_l", n4)
         n5_l = load_list("n5_l", n5)
 
-        def window(name, width, tag=None):
-            tile = sb(name, [P, width], F32, tag=tag)
+        def window(name, width):
+            tile = sb(name, [P, width], F32)
             nc.vector.memset(tile[:, N:], 0.0)
             return tile
-
 
         def pick_words(name, lst, tag=None):
             words = sb(name, [P, S], U32, tag=tag)
@@ -83,20 +97,21 @@ def tile_picked_mombgsumglseover_none_p_kernel(
             return words
 
         def pick_scales(name, lst, tag=None):
-            picked = sb(name + "_listed", [P, S], U8, tag=tag)
+            picked = sb(name, [P, S], U8, tag=tag)
             nc.vector.tensor_copy(picked[:], table_scales[:].indirect(lst[:]))
-            dealt = sb(name, [P, S], U8)
-            nc.vector.tensor_copy(
-                dealt[:].rearrange("p (t m) -> p t m", t=PACK),
-                picked[:].rearrange("p (m t) -> p t m", t=PACK),
-            )
-            return dealt
+            return picked
 
-        def weave_views(dst, src):
-            return (
-                dst.rearrange("p (c i t) -> p c t i", i=4, t=PACK),
-                src.rearrange("p t (c i) -> p c t i", i=4),
+        def deal_scales(dealt, picked, tiles):
+            nc.vector.tensor_copy(
+                dealt[:].rearrange("p (t m) -> p t m", t=PACK)[:, tiles, :],
+                picked[:].rearrange("p (m t) -> p t m", t=PACK)[:, tiles, :],
             )
+
+        def weave(copy, dst, src):
+            copy(dst.rearrange("p (c i r) -> p c r i", i=4, r=PACK), src.rearrange("p r (c i) -> p c r i", i=4))
+
+        def quantise(codes, scales, woven):
+            nc.vector.quantize_mx(codes.bitcast(FP8X4), scales, woven)
 
         def gather(dst, win, lst):
             nc.scalar.activation(dst, win.indirect(lst), ACT.Copy)
@@ -107,231 +122,232 @@ def tile_picked_mombgsumglseover_none_p_kernel(
                 rhs=rhs.bitcast(FP8X4), rhs_scale=rhs_scale, start=True, stop=True,
             )
 
-        xa_scales = pick_scales("xa_scales", offs_l)
-        xa_words = pick_words("xa_words", offs_l)
-        a_win = [window("a_win%d" % t, 2 * H + PAD) for t in range(PACK)]
-        ex_win = [window("ex_win%d" % t, N + PAD) for t in range(PACK - 1)]
-        gb_win = [window("gb_win%d" % t, N + PAD) for t in range(PACK)]
-        wa_codes = sb("wa_codes", [P, H], U32)
-        wa_scales = sb("wa_scales", [P, H], U8)
-        parts = ((0, 0, HALF, nc.vector.tensor_copy), (1, 0, P, nc.vector.tensor_copy), (1, P, HALF, nc.scalar.copy))
-        for i, (u, c0, c1, copy) in enumerate(parts):
-            woven = sb("wa_woven%d" % i, [P, PACK * (c1 - c0)], BF16)
-            dst, src = weave_views(woven[:], wa_raw[u][:, :, c0:c1])
-            copy(dst, src)
-            cols = slice(u * HALF + c0, u * HALF + c1)
-            nc.vector.quantize_mx(wa_codes[:, cols].bitcast(FP8X4), wa_scales[:, cols], woven[:])
-        for i, (u, c0, c1, copy) in enumerate(parts):
-            cols = slice(u * HALF + c0, u * HALF + c1)
-            acc = psum.tile([P, c1 - c0], F32, name="a_first%d" % i, tag="bank%d" % i)
-            mx_pass(acc[:], xa_words[:, :P], xa_scales[:, :P], wa_codes[:, cols], wa_scales[:, cols])
-            (nc.scalar.copy if i == 0 else nc.vector.tensor_copy)(a_win[0][:, cols], acc[:])
-        for t in range(1, PACK):
-            acc = psum.tile([P, H], F32, name="a_acc%d" % t, tag="bank%d" % (PACK + t))
-            rows = slice(t * P, (t + 1) * P)
-            mx_pass(acc[:], xa_words[:, rows], xa_scales[:, rows], wa_codes[:], wa_scales[:])
-            nc.vector.tensor_copy(a_win[t][:, :H], acc[:])
-        half_gt = sb("half_gt", [P, PACK], F32)
-        nc.vector.tensor_scalar(half_gt[:], gt_cols[:], 0.5, None, ALU.mult)
-
-        z_rows = sb("z_rows", [P, PACK, H], BF16)
-
-        def n1_gather(t):
-            mb = sb("mb%d" % t, [P, W], F32)
-            for q in range(2):
-                gather(mb[:, q * 1024 : (q + 1) * 1024], a_win[t][:], n1_l[:, q * 64 : (q + 1) * 64])
-            return mb
-
-        def sums(t, mb):
-            ms = sb("ms%d" % t, [P, H], F32, tag="hold%d" % t)
-            for q in range(2):
-                nc.vector.tensor_reduce(
-                    ms[:, q * HALF : (q + 1) * HALF],
-                    mb[:, q * 1024 : (q + 1) * 1024].rearrange("p (j f) -> p j f", f=4), AX.X, ALU.add,
-                )
-            return ms
-
-        def tanh_step(t, ms):
-            th = sb("th%d" % t, [P, H], F32)
-            nc.scalar.activation(th[:], ms[:], ACT.Tanh, scale=0.5)
-            return th
-
-        def z_step(t, th):
-            gate = sb("gate%d" % t, [P, H], F32)
-            col = half_gt[:, t : t + 1]
-            nc.vector.tensor_scalar(gate[:], th[:], col, col, ALU.mult, ALU.add)
-            nc.vector.tensor_tensor(z_rows[:, t, :], a_win[t][:, :H], gate[:], ALU.mult)
-
-        mb0 = n1_gather(0)
-        mb1 = n1_gather(1)
-        th0 = tanh_step(0, sums(0, mb0))
-        mb2 = n1_gather(2)
-        xb_words = pick_words("xb_words", two_l, tag="wa_codes")
-        xb_scales = pick_scales("xb_scales", two_l, tag="wa_scales")
-        th1 = tanh_step(1, sums(1, mb1))
-        mb3 = n1_gather(3)
-        wb_woven = sb("wb_woven", [P, PACK * N], BF16, tag="xa_words")
-        dst, src = weave_views(wb_woven[:], wb_raw[:])
-        nc.vector.tensor_copy(dst, src)
-        wb_codes = sb("wb_codes", [P, N], U32)
-        wb_scales = sb("wb_scales", [P, N], U8)
-        nc.vector.quantize_mx(wb_codes[:].bitcast(FP8X4), wb_scales[:], wb_woven[:])
-        b_acc = []
-        for t in range(PACK):
-            acc = psum.tile([P, N], F32, name="b_acc%d" % t, tag="bank%d" % t)
-            rows = slice(t * P, (t + 1) * P)
-            mx_pass(acc[:], xb_words[:, rows], xb_scales[:, rows], wb_codes[:], wb_scales[:])
-            b_acc.append(acc)
-        cv_win = [window("cv_win%d" % c, 2 * N, tag=old) for c, old in enumerate(("mb0", "mb1", "wb_raw", "xa_words"))]
-        th2 = tanh_step(2, sums(2, mb2))
-        z_step(0, th0)
-        th3 = tanh_step(3, sums(3, mb3))
-        ex_win.append(window("ex_win3", N + PAD, tag="mb3"))
-
-        ex_sum = sb("ex_sum", [P, N // P, PACK, P], F32)
-        ex_n2 = sb("ex_n2", [P, PACK, N], F32, tag="hold3")
-
         def by_quarter(ap):
             return ap.rearrange("p (q j) -> p q j", j=P)
 
+        def tile_columns(first, end):
+            return slice(first * P, end * P)
+
+        xb_listed = pick_scales("xb_listed", two_l)
+        xb_scales = sb("xb_scales", [P, S], U8)
+        deal_scales(xb_scales, xb_listed, slice(0, PACK))
+        xb_words = pick_words("xb_words", two_l)
+        ex_win = [window("ex_win%d" % t, N + PAD) for t in range(PACK)]
+        gb_win = [window("gb_win%d" % t, N + PAD) for t in range(PACK)]
+        a_win = [window("a_win%d" % t, W // 2 + PAD) for t in range(PACK)]
+        wb_codes = sb("wb_codes", [P, N], U32)
+        wb_scales = sb("wb_scales", [P, N], U8)
+        wb_parts = ((0, 0, HALF, nc.vector.tensor_copy), (1, 0, P, nc.vector.tensor_copy), (1, P, HALF, nc.scalar.copy))
+        for i, (u, c0, c1, copy) in enumerate(wb_parts):
+            woven = sb("wb_woven%d" % i, [P, PACK * (c1 - c0)], BF16)
+            weave(copy, woven[:], wb_raw[u][:, :, c0:c1])
+            cols = slice(u * HALF + c0, u * HALF + c1)
+            quantise(wb_codes[:, cols], wb_scales[:, cols], woven[:])
+        b_acc = [bank("b_acc%d" % t, N, t) for t in range(PACK)]
+        b_first_hi = bank("b_first_hi", N, PACK)
+
+        def b_bank(t, cols):
+            return b_first_hi if t == 0 and cols == HI else b_acc[t]
+
+        def b_step(t, cols, pieces):
+            rows = tile_columns(t, t + 1)
+            acc = b_bank(t, cols)
+            for piece in pieces:
+                mx_pass(acc[:, piece], xb_words[:, rows], xb_scales[:, rows], wb_codes[:, piece], wb_scales[:, piece])
+            nc.scalar.activation(ex_win[t][:, cols], acc[:, cols], ACT.Exp)
+
+        ex_n2 = sb("ex_n2", [P, PACK, N], F32)
+        b_step(0, LO, [LO])
+        b_step(0, HI, [tile_columns(2, 3), tile_columns(3, 4)])
+        for t in range(1, PACK):
+            b_step(t, LO, [LO])
+        for t in range(PACK):
+            if t < LAST:
+                b_step(t + 1, HI, [HI])
+            gather(ex_n2[:, t, :], ex_win[t][:], n2_l[:])
+
+        xa_words = pick_words("xa_words", offs_l, tag="xb_scales")
+        xa_listed = pick_scales("xa_listed", offs_l, tag="wb_woven2")
+        xa_scales = sb("xa_scales", [P, S], U8)
+        deal_scales(xa_scales, xa_listed, slice(0, 1))
+        wa_woven = sb("wa_woven", [P, PACK * H], BF16)
+        weave(nc.vector.tensor_copy, wa_woven[:], wa_raw[:])
+        wa_codes = sb("wa_codes", [P, H], U32)
+        wa_scales = sb("wa_scales", [P, H], U8)
+        quantise(wa_codes[:], wa_scales[:], wa_woven[:])
+
+        gi_cols = load_weights_of_places("gi_cols", gi, tag="wa_woven")
+
         def gb_step(t):
-            nc.vector.tensor_scalar(gb_win[t][:, :N], b_acc[t][:], gi_cols[:, t : t + 1], None, ALU.mult)
+            for cols in ((LO, HI) if t == 0 else (WHOLE,)):
+                nc.vector.tensor_scalar(
+                    gb_win[t][:, cols], b_bank(t, cols)[:, cols], gi_cols[:, t : t + 1], None, ALU.mult
+                )
+
+        def a_step(t, cols, number):
+            acc = bank("a_acc%d" % number, cols.stop - cols.start, number)
+            rows = tile_columns(t, t + 1)
+            mx_pass(acc[:], xa_words[:, rows], xa_scales[:, rows], wa_codes[:, cols], wa_scales[:, cols])
+            nc.vector.tensor_copy(a_win[t][:, cols], acc[:])
+
+        a_step(0, LO, 5)
+        a_step(0, HI, 6)
+        deal_scales(xa_scales, xa_listed, slice(1, PACK))
+        a_step(1, WHOLE, 7)
+        gb_step(0)
+        a_step(2, WHOLE, PACK)
+        a_step(3, WHOLE, 0)
+        ex_sum = sb("ex_sum", [P, N // P, PACK, P], F32, tag="xb_scales")
+        half_gt = sb("half_gt", [P, PACK], F32)
+        nc.vector.tensor_scalar(half_gt[:], gt_cols[:], 0.5, None, ALU.mult)
 
         def add_step(t):
             nc.vector.tensor_tensor(
                 ex_sum[:, :, t, :], by_quarter(ex_win[t][:, :N]), by_quarter(ex_n2[:, t, :]), ALU.add
             )
 
-        for t in range(PACK):
-            nc.scalar.activation(ex_win[t][:, :N], b_acc[t][:], ACT.Exp)
-        for t in range(PACK):
-            gather(ex_n2[:, t, :], ex_win[t][:], n2_l[:])
-        gb_step(0)
-        gb_step(1)
-        for t, th in ((1, th1), (2, th2), (3, th3)):
-            z_step(t, th)
-        gb_step(2)
-        gb_step(3)
-        add_step(0)
-        add_step(1)
-        z_woven = sb("z_woven", [P, PACK * H], BF16)
-        nc.vector.tensor_copy(
-            z_woven[:].rearrange("p (c m t) -> p c m t", c=PACK, t=PACK),
-            z_rows[:].rearrange("p t (m c) -> p c m t", c=PACK),
-        )
-        add_step(2)
-        add_step(3)
-        z_codes = sb("z_codes", [P, H], U32)
-        z_scales = sb("z_scales", [P, H], U8)
-        nc.vector.quantize_mx(z_codes[:].bitcast(FP8X4), z_scales[:], z_woven[:])
+        z_rows = sb("z_rows", [P, PACK, H], BF16)
 
-        chunks = (slice(0, 256), slice(256, 384), slice(384, 512))
+        def n1_pieces(t):
+            cuts = N1_CUTS if t < LAST else N1_CUTS_LAST
+            return zip(cuts, cuts[1:])
+
+        def n1_gather(t):
+            mb = sb("mb%d" % t, [P, W], F32)
+            for q0, q1 in n1_pieces(t):
+                gather(mb[:, q0:q1], a_win[t][:], entries(n1_l, q0, q1))
+            return mb
+
+        def sum_members(t, mb):
+            ms = sb("ms%d" % t, [P, H], F32)
+            for q0, q1 in n1_pieces(t):
+                nc.vector.tensor_reduce(
+                    ms[:, q0 // MEMBERS : q1 // MEMBERS],
+                    mb[:, q0:q1].rearrange("p (j f) -> p j f", f=MEMBERS), AX.X, ALU.add,
+                )
+            return ms
+
+        cv_win = [sb("cv_win%d" % c, [P, 2 * N], F32) for c in range(PACK)]
+
+        def tanh_step(t, ms):
+            th = cv_win[t][:, N:]
+            nc.scalar.activation(th, ms[:], ACT.Tanh, scale=0.5)
+            return th
+
+        def z_step(t, th):
+            gate = sb("gate%d" % t, [P, H], F32)
+            col = half_gt[:, t : t + 1]
+            nc.vector.tensor_scalar(gate[:], th, col, col, ALU.mult, ALU.add)
+            nc.vector.tensor_tensor(z_rows[:, t, :], a_win[t][:, :H], gate[:], ALU.mult)
+
         gb_n3 = {}
 
         def n3_gather(k, t, dst):
-            cols = chunks[k]
-            gather(dst, gb_win[t][:], n3_l[:, cols.start // 16 : cols.stop // 16])
+            gather(dst, gb_win[t][:], entries(n3_l, CHUNKS[k].start, CHUNKS[k].stop))
             gb_n3[(k, t)] = dst
 
-        gb_early = sb("gb_early", [P, PACK, HALF], F32)
-        for t in range(PACK):
-            n3_gather(0, t, gb_early[:, t, :])
+        mb0 = n1_gather(0)
+        mb1 = n1_gather(1)
+        for t in range(1, PACK):
+            gb_step(t)
+        th0 = tanh_step(0, sum_members(0, mb0))
+        mb2 = n1_gather(2)
+        add_step(0)
+        add_step(1)
+        th1 = tanh_step(1, sum_members(1, mb1))
+        mb3 = n1_gather(3)
+        add_step(2)
+        add_step(3)
+        th2 = tanh_step(2, sum_members(2, mb2))
+        gb_first = sb("gb_first", [P, HALF], F32, tag="mb2")
+        n3_gather(0, 0, gb_first[:])
+        z_step(0, th0)
+        th3 = tanh_step(3, sum_members(3, mb3))
+        for t, th in ((1, th1), (2, th2), (3, th3)):
+            z_step(t, th)
+        z_codes = sb("z_codes", [P, H], U32)
+        z_scales = sb("z_scales", [P, H], U8)
 
-        lse_lo = sb("lse_lo", [P, PACK, HALF], F32)
-        lse_hi = sb("lse_hi", [P, 2, PACK, P], F32)
+        def z_quantise(c0, c1, tag=None):
+            woven = sb("z_woven%d" % c0, [P, (c1 - c0) * PACK * P], BF16, tag=tag)
+            nc.vector.tensor_copy(
+                woven[:].rearrange("p (c m t) -> p c m t", m=P, t=PACK),
+                z_rows[:].rearrange("p t (m c) -> p c m t", c=PACK)[:, c0:c1],
+            )
+            cols = tile_columns(c0, c1)
+            quantise(z_codes[:, cols], z_scales[:, cols], woven[:])
+
+        z_quantise(0, 2)
+
+        gb_early = sb("gb_early", [P, LAST, HALF], F32, tag="mb3")
+        for t in range(1, PACK):
+            n3_gather(0, t, gb_early[:, t - 1, :])
+
+        lse = sb("lse", [P, PACK * N], F32, tag="gate3")
+        lse_lo = lse[:, : PACK * HALF].rearrange("p (t j) -> p t j", t=PACK)
+        lse_hi = lse[:, PACK * HALF :].rearrange("p (q t j) -> p q t j", q=2, t=PACK)
         for t in range(PACK):
             nc.scalar.activation(by_quarter(lse_lo[:, t, :]), ex_sum[:, :2, t, :], ACT.Ln)
-        nc.scalar.activation(lse_hi[:], ex_sum[:, 2:], ACT.Ln)
+        nc.scalar.activation(lse_hi, ex_sum[:, 2:], ACT.Ln)
 
-        z2_rows = [sb("z2_rows%d" % k, [P, PACK, c.stop - c.start], BF16) for k, c in enumerate(chunks)]
-        z2_woven = [sb("z2_woven%d" % k, [P, PACK * (c.stop - c.start)], BF16) for k, c in enumerate(chunks)]
+        z2_rows = [sb("z2_rows%d" % k, [P, PACK, c.stop - c.start], BF16) for k, c in enumerate(CHUNKS)]
+        z2_woven = [sb("z2_woven%d" % k, [P, PACK * (c.stop - c.start)], BF16) for k, c in enumerate(CHUNKS)]
         z2_codes = sb("z2_codes", [P, N], U32)
         z2_scales = sb("z2_scales", [P, N], U8)
-        first_acc = [
-            psum.tile([P, c.stop - c.start], F32, name="first_acc%d" % k, tag="bank%d" % (PACK + k))
-            for k, c in enumerate(chunks)
-        ]
+        first_acc = [bank("first_acc%d" % k, c.stop - c.start, PACK + k) for k, c in enumerate(CHUNKS)]
 
-        def z2_step(k, t, direct=False):
-            cols = chunks[k]
-            dst, looked_up = z2_rows[k][:, t, :], gb_n3[(k, t)]
-            if direct:
-                dst = z2_woven[k][:].rearrange("p (j t) -> p t j", t=PACK)[:, t, :]
-            if k == 0:
-                log_sum = lse_lo[:, t, :]
-            elif cols.stop - cols.start == P:
-                log_sum = lse_hi[:, cols.start // P - 2, t, :]
-            else:
-                log_sum, dst, looked_up = lse_hi[:, :, t, :], by_quarter(dst), by_quarter(looked_up)
-            nc.vector.scalar_tensor_tensor(dst, log_sum, gi_cols[:, t : t + 1], looked_up, ALU.mult, ALU.subtract)
-
-        def z2_weave(k, rows=PACK):
-            dst, src = weave_views(z2_woven[k][:], z2_rows[k][:])
-            nc.vector.tensor_copy(dst[:, :, :rows, :], src[:, :, :rows, :])
-
-        def cv_products(k):
-            cols = chunks[k]
-            nc.vector.quantize_mx(z2_codes[:, cols].bitcast(FP8X4), z2_scales[:, cols], z2_woven[k][:])
+        def z2_chunk(k):
+            cols = CHUNKS[k]
+            for t in range(PACK):
+                nc.vector.scalar_tensor_tensor(
+                    z2_rows[k][:, t, :], lse_lo[:, t, :] if k == 0 else lse_hi[:, k - 1, t, :],
+                    gi_cols[:, t : t + 1], gb_n3[(k, t)], ALU.mult, ALU.subtract,
+                )
+            weave(nc.vector.tensor_copy, z2_woven[k][:], z2_rows[k][:])
+            quantise(z2_codes[:, cols], z2_scales[:, cols], z2_woven[k][:])
             mx_pass(first_acc[k][:], z_codes[:, :P], z_scales[:, :P], z2_codes[:, cols], z2_scales[:, cols])
 
-        def cv_rest(c):
-            rows = slice(c * P, (c + 1) * P)
-            acc = psum.tile([P, N], F32, name="cv_acc%d" % c, tag="bank%d" % c)
+        spent = [ex_sum[:, q, LAST, :] for q in range(2)] + [ex_sum[:, q, t, :] for q in (2, 3) for t in range(PACK)]
+        z2_chunk(0)
+        for k in (1, 2):
+            for t in range(PACK):
+                n3_gather(k, t, spent[PACK * (k - 1) + t])
+            z2_chunk(k)
+
+        for k, cols in enumerate(CHUNKS):
+            nc.scalar.activation(cv_win[0][:, cols], first_acc[k][:], ACT.Copy, scale=0.0625)
+
+        def cv_step(c):
+            rows = tile_columns(c, c + 1)
+            acc = bank("cv_acc%d" % c, N, c)
             mx_pass(acc[:], z_codes[:, rows], z_scales[:, rows], z2_codes[:], z2_scales[:])
             nc.vector.tensor_scalar(cv_win[c][:, :N], acc[:], 0.0625, None, ALU.mult)
 
-        spent = ex_sum[:].rearrange("p q t j -> p (q t j)")
-        for t in range(PACK):
-            z2_step(0, t)
-        z2_weave(0)
-        cv_products(0)
-        for t, at in enumerate((3, 7, 8, 9)):
-            n3_gather(1, t, spent[:, at * P : at * P + 128])
-        for t in range(PACK):
-            z2_step(1, t)
-        z2_weave(1)
-        cv_products(1)
-        for t, at in enumerate((10, 11, 12, 13)):
-            n3_gather(2, t, spent[:, at * P : at * P + 128])
-        for t in range(PACK):
-            z2_step(2, t)
-        z2_weave(2)
-        cv_products(2)
-        for k in range(2):
-            nc.scalar.activation(cv_win[0][:, chunks[k]], first_acc[k][:], ACT.Copy, scale=0.0625)
-        nc.vector.tensor_scalar(cv_win[0][:, chunks[2]], first_acc[2][:], 0.0625, None, ALU.mult)
-        for c in range(1, PACK):
-            cv_rest(c)
+        cv_step(1)
+        z_quantise(2, PACK, tag="z2_woven2")
+        cv_step(2)
+        cv_step(3)
 
-        g4 = [sb("g4_%d" % c, [P, N], F32) for c in range(PACK)]
-        g5 = [sb("g5_%d" % c, [P, N], F32) for c in range(PACK)]
-        top = {}
+        cv_n4 = [sb("cv_n4_%d" % c, [P, N], F32) for c in range(PACK)]
+        cv_n5 = [sb("cv_n5_%d" % c, [P, N], F32) for c in range(PACK)]
         res = [sb("res%d" % c, [P, N], F32) for c in range(PACK)]
         out_rows = out.rearrange("(p c) n -> c p n", c=PACK)
 
-        def cv_gather(c, cols):
-            lst = slice(cols.start // 16, cols.stop // 16)
-            gather(g4[c][:, cols], cv_win[c][:], n4_l[:, lst])
-            gather(g5[c][:, cols], cv_win[c][:], n5_l[:, lst])
+        def finish(c, parts):
+            top = sb("top%d" % c, [P, N], F32, tag="top")
+            for cols in parts:
+                nc.vector.tensor_tensor(top[:, cols], cv_n4[c][:, cols], cv_n5[c][:, cols], ALU.max)
+                nc.vector.scalar_tensor_tensor(
+                    res[c][:, cols], cv_win[c][:, cols], -0.75, top[:, cols], ALU.mult, ALU.add
+                )
+                nc.sync.dma_start(out_rows[c][:, cols], res[c][:, cols])
 
-        def finish(c, cols):
-            if c not in top:
-                top[c] = sb("top%d" % c, [P, N], F32, tag="top")
-            nc.vector.tensor_tensor(top[c][:, cols], g4[c][:, cols], g5[c][:, cols], ALU.max)
-            nc.vector.scalar_tensor_tensor(
-                res[c][:, cols], cv_win[c][:, cols], -0.75, top[c][:, cols], ALU.mult, ALU.add
-            )
-            nc.sync.dma_start(out_rows[c][:, cols], res[c][:, cols])
-
-        whole = slice(0, N)
-        cv_gather(0, whole)
-        cv_gather(1, whole)
-        finish(0, whole)
-        cv_gather(2, whole)
-        finish(1, whole)
-        gather(g4[3][:], cv_win[3][:], n4_l[:])
-        finish(2, whole)
-        gather(g5[3][:, :HALF], cv_win[3][:], n5_l[:, :16])
-        gather(g5[3][:, HALF:], cv_win[3][:], n5_l[:, 16:])
-        finish(3, slice(0, HALF))
-        finish(3, slice(HALF, N))
+        for c in range(PACK):
+            gather(cv_n4[c][:], cv_win[c][:], n4_l[:])
+            if c < LAST:
+                gather(cv_n5[c][:], cv_win[c][:], n5_l[:])
+            if c > 0:
+                finish(c - 1, (WHOLE,))
+        for cols in (LO, HI):
+            gather(cv_n5[LAST][:, cols], cv_win[LAST][:], entries(n5_l, cols.start, cols.stop))
+        finish(LAST, (LO, HI))

from contextlib import ExitStack

import concourse.mybir as mybir

K, T, S, N, H, W = 512, 2048, 512, 512, 512, 2048
FLOPS = 2 * (K * S * H + K * S * N + S * H * N)

F32 = mybir.dt.float32
BF16 = mybir.dt.bfloat16
I32 = mybir.dt.int32
U32 = mybir.dt.uint32
U16 = mybir.dt.uint16
U8 = mybir.dt.uint8
FP8X4 = mybir.dt.float8_e4m3fn_x4
ALU = mybir.AluOpType
ACT = mybir.ActivationFunctionType
AX = mybir.AxisListType

P = 128
PACK = 4
LAST = PACK - 1
MEMBERS = W // H
PER_COLUMN = 16
PAD = 16
HALF = N // 2
LO, HI, WHOLE = slice(0, HALF), slice(HALF, N), slice(0, N)
N1_CUTS = (0, W // 2, W)
N1_CUTS_LAST = (0, W // 2, W - HALF, W)
CHUNKS = (slice(0, HALF), slice(HALF, HALF + P), slice(HALF + P, N))


def tile_picked_mombgsumglseover_none_p_kernel(
    tc, x_words, x_scales, wa, wb, gt, gi, offs, two, n1, n2, n3, n4, n5, out
):
    nc = tc.nc
    with ExitStack() as ctx:
        held = ctx.enter_context(tc.tile_pool(name="held", bufs=1))
        psum = ctx.enter_context(tc.psum_pool(name="psum", bufs=1))

        def sb(name, shape, dtype, tag=None):
            return held.tile(shape, dtype, name=name, tag=tag or name, align_bytes=64)

        def bank(name, width, number):
            return psum.tile([P, width], F32, name=name, tag="bank%d" % number)

        def load_list(name, src):
            tile = sb(name, list(src.shape), U16)
            nc.sync.dma_start(tile[:], src)
            return tile

        def load_weights_of_places(name, src, tag=None):
            tile = sb(name, [P, PACK], F32, tag=tag)
            nc.sync.dma_start(tile[:], src.rearrange("(p t) o -> p (t o)", t=PACK))
            return tile

        def entries(lst, first, end):
            return lst[:, first // PER_COLUMN : end // PER_COLUMN]

        table_scales = sb("table_scales", [P, T], U8)
        nc.vector.memset(table_scales[:].bitcast(I32), 0)

        two_l = load_list("two_l", two)
        n2_l = load_list("n2_l", n2)
        offs_l = load_list("offs_l", offs)
        for q in range(4):
            nc.sync.dma_start(
                table_scales[32 * q : 32 * q + 4, :].bitcast(I32),
                x_scales[0, 4 * q : 4 * q + 4, :].bitcast(I32),
            )
        table_words = sb("table_words", [P, T], I32)
        nc.sync.dma_start(table_words[:], x_words[0].rearrange("p c r -> p (c r)").bitcast(I32))
        wb_rows = wb.rearrange("(p j) n -> p j n", j=PACK)
        wb_raw = []
        for u, cols in enumerate((LO, HI)):
            raw = sb("wb_raw%d" % u, [P, PACK, HALF], F32)
            nc.sync.dma_start(raw[:], wb_rows[:, :, cols])
            wb_raw.append(raw)
        wa_raw = sb("wa_raw", [P, PACK, H], F32)
        nc.sync.dma_start(wa_raw[:], wa.rearrange("(p j) n -> p j n", j=PACK))
        n1_l = load_list("n1_l", n1)
        gt_cols = load_weights_of_places("gt_cols", gt)
        n3_l = load_list("n3_l", n3)
        n4_l = load_list("n4_l", n4)
        n5_l = load_list("n5_l", n5)

        def window(name, width):
            tile = sb(name, [P, width], F32)
            nc.vector.memset(tile[:, N:], 0.0)
            return tile

        def pick_words(name, lst, tag=None):
            words = sb(name, [P, S], U32, tag=tag)
            nc.vector.tensor_copy(
                words[:].rearrange("p (t m) -> p m t", t=PACK),
                table_words[:].bitcast(U32).indirect(lst[:]),
            )
            return words

        def pick_scales(name, lst, tag=None):
            picked = sb(name, [P, S], U8, tag=tag)
            nc.vector.tensor_copy(picked[:], table_scales[:].indirect(lst[:]))
            return picked

        def deal_scales(dealt, picked, tiles):
            nc.vector.tensor_copy(
                dealt[:].rearrange("p (t m) -> p t m", t=PACK)[:, tiles, :],
                picked[:].rearrange("p (m t) -> p t m", t=PACK)[:, tiles, :],
            )

        def weave(copy, dst, src):
            copy(dst.rearrange("p (c i r) -> p c r i", i=4, r=PACK), src.rearrange("p r (c i) -> p c r i", i=4))

        def quantise(codes, scales, woven):
            nc.vector.quantize_mx(codes.bitcast(FP8X4), scales, woven)

        def gather(dst, win, lst):
            nc.scalar.activation(dst, win.indirect(lst), ACT.Copy)

        def mx_pass(acc, lhs, lhs_scale, rhs, rhs_scale):
            nc.tensor.matmul_mx(
                out=acc, lhsT=lhs.bitcast(FP8X4), lhsT_scale=lhs_scale,
                rhs=rhs.bitcast(FP8X4), rhs_scale=rhs_scale, start=True, stop=True,
            )

        def by_quarter(ap):
            return ap.rearrange("p (q j) -> p q j", j=P)

        def tile_columns(first, end):
            return slice(first * P, end * P)

        xb_listed = pick_scales("xb_listed", two_l)
        xb_scales = sb("xb_scales", [P, S], U8)
        deal_scales(xb_scales, xb_listed, slice(0, PACK))
        xb_words = pick_words("xb_words", two_l)
        ex_win = [window("ex_win%d" % t, N + PAD) for t in range(PACK)]
        gb_win = [window("gb_win%d" % t, N + PAD) for t in range(PACK)]
        a_win = [window("a_win%d" % t, W // 2 + PAD) for t in range(PACK)]
        wb_codes = sb("wb_codes", [P, N], U32)
        wb_scales = sb("wb_scales", [P, N], U8)
        wb_parts = ((0, 0, HALF, nc.vector.tensor_copy), (1, 0, P, nc.vector.tensor_copy), (1, P, HALF, nc.scalar.copy))
        for i, (u, c0, c1, copy) in enumerate(wb_parts):
            woven = sb("wb_woven%d" % i, [P, PACK * (c1 - c0)], BF16)
            weave(copy, woven[:], wb_raw[u][:, :, c0:c1])
            cols = slice(u * HALF + c0, u * HALF + c1)
            quantise(wb_codes[:, cols], wb_scales[:, cols], woven[:])
        b_acc = [bank("b_acc%d" % t, N, t) for t in range(PACK)]
        b_first_hi = bank("b_first_hi", N, PACK)

        def b_bank(t, cols):
            return b_first_hi if t == 0 and cols == HI else b_acc[t]

        def b_step(t, cols, pieces):
            rows = tile_columns(t, t + 1)
            acc = b_bank(t, cols)
            for piece in pieces:
                mx_pass(acc[:, piece], xb_words[:, rows], xb_scales[:, rows], wb_codes[:, piece], wb_scales[:, piece])
            nc.scalar.activation(ex_win[t][:, cols], acc[:, cols], ACT.Exp)

        ex_n2 = sb("ex_n2", [P, PACK, N], F32)
        b_step(0, LO, [LO])
        b_step(0, HI, [tile_columns(2, 3), tile_columns(3, 4)])
        for t in range(1, PACK):
            b_step(t, LO, [LO])
        for t in range(PACK):
            if t < LAST:
                b_step(t + 1, HI, [HI])
            gather(ex_n2[:, t, :], ex_win[t][:], n2_l[:])

        xa_words = pick_words("xa_words", offs_l, tag="xb_scales")
        xa_listed = pick_scales("xa_listed", offs_l, tag="wb_woven2")
        xa_scales = sb("xa_scales", [P, S], U8)
        deal_scales(xa_scales, xa_listed, slice(0, 1))
        wa_woven = sb("wa_woven", [P, PACK * H], BF16)
        weave(nc.vector.tensor_copy, wa_woven[:], wa_raw[:])
        wa_codes = sb("wa_codes", [P, H], U32)
        wa_scales = sb("wa_scales", [P, H], U8)
        quantise(wa_codes[:], wa_scales[:], wa_woven[:])

        gi_cols = load_weights_of_places("gi_cols", gi, tag="wa_woven")

        def gb_step(t):
            for cols in ((LO, HI) if t == 0 else (WHOLE,)):
                nc.vector.tensor_scalar(
                    gb_win[t][:, cols], b_bank(t, cols)[:, cols], gi_cols[:, t : t + 1], None, ALU.mult
                )

        def a_step(t, cols, number):
            acc = bank("a_acc%d" % number, cols.stop - cols.start, number)
            rows = tile_columns(t, t + 1)
            mx_pass(acc[:], xa_words[:, rows], xa_scales[:, rows], wa_codes[:, cols], wa_scales[:, cols])
            nc.vector.tensor_copy(a_win[t][:, cols], acc[:])

        a_step(0, LO, 5)
        a_step(0, HI, 6)
        deal_scales(xa_scales, xa_listed, slice(1, PACK))
        a_step(1, WHOLE, 7)
        gb_step(0)
        a_step(2, WHOLE, PACK)
        a_step(3, WHOLE, 0)
        ex_sum = sb("ex_sum", [P, N // P, PACK, P], F32, tag="xb_scales")
        half_gt = sb("half_gt", [P, PACK], F32)
        nc.vector.tensor_scalar(half_gt[:], gt_cols[:], 0.5, None, ALU.mult)

        def add_step(t):
            nc.vector.tensor_tensor(
                ex_sum[:, :, t, :], by_quarter(ex_win[t][:, :N]), by_quarter(ex_n2[:, t, :]), ALU.add
            )

        z_rows = sb("z_rows", [P, PACK, H], BF16)

        def n1_pieces(t):
            cuts = N1_CUTS if t < LAST else N1_CUTS_LAST
            return zip(cuts, cuts[1:])

        def n1_gather(t):
            mb = sb("mb%d" % t, [P, W], F32)
            for q0, q1 in n1_pieces(t):
                gather(mb[:, q0:q1], a_win[t][:], entries(n1_l, q0, q1))
            return mb

        def sum_members(t, mb):
            ms = sb("ms%d" % t, [P, H], F32)
            for q0, q1 in n1_pieces(t):
                nc.vector.tensor_reduce(
                    ms[:, q0 // MEMBERS : q1 // MEMBERS],
                    mb[:, q0:q1].rearrange("p (j f) -> p j f", f=MEMBERS), AX.X, ALU.add,
                )
            return ms

        cv_win = [sb("cv_win%d" % c, [P, 2 * N], F32) for c in range(PACK)]

        def tanh_step(t, ms):
            th = cv_win[t][:, N:]
            nc.scalar.activation(th, ms[:], ACT.Tanh, scale=0.5)
            return th

        def z_step(t, th):
            gate = sb("gate%d" % t, [P, H], F32)
            col = half_gt[:, t : t + 1]
            nc.vector.tensor_scalar(gate[:], th, col, col, ALU.mult, ALU.add)
            nc.vector.tensor_tensor(z_rows[:, t, :], a_win[t][:, :H], gate[:], ALU.mult)

        gb_n3 = {}

        def n3_gather(k, t, dst):
            gather(dst, gb_win[t][:], entries(n3_l, CHUNKS[k].start, CHUNKS[k].stop))
            gb_n3[(k, t)] = dst

        mb0 = n1_gather(0)
        mb1 = n1_gather(1)
        for t in range(1, PACK):
            gb_step(t)
        th0 = tanh_step(0, sum_members(0, mb0))
        mb2 = n1_gather(2)
        add_step(0)
        add_step(1)
        th1 = tanh_step(1, sum_members(1, mb1))
        mb3 = n1_gather(3)
        add_step(2)
        add_step(3)
        th2 = tanh_step(2, sum_members(2, mb2))
        gb_first = sb("gb_first", [P, HALF], F32, tag="mb2")
        n3_gather(0, 0, gb_first[:])
        z_step(0, th0)
        th3 = tanh_step(3, sum_members(3, mb3))
        for t, th in ((1, th1), (2, th2), (3, th3)):
            z_step(t, th)
        z_codes = sb("z_codes", [P, H], U32)
        z_scales = sb("z_scales", [P, H], U8)

        def z_quantise(c0, c1, tag=None):
            woven = sb("z_woven%d" % c0, [P, (c1 - c0) * PACK * P], BF16, tag=tag)
            nc.vector.tensor_copy(
                woven[:].rearrange("p (c m t) -> p c m t", m=P, t=PACK),
                z_rows[:].rearrange("p t (m c) -> p c m t", c=PACK)[:, c0:c1],
            )
            cols = tile_columns(c0, c1)
            quantise(z_codes[:, cols], z_scales[:, cols], woven[:])

        z_quantise(0, 2)

        gb_early = sb("gb_early", [P, LAST, HALF], F32, tag="mb3")
        for t in range(1, PACK):
            n3_gather(0, t, gb_early[:, t - 1, :])

        lse = sb("lse", [P, PACK * N], F32, tag="gate3")
        lse_lo = lse[:, : PACK * HALF].rearrange("p (t j) -> p t j", t=PACK)
        lse_hi = lse[:, PACK * HALF :].rearrange("p (q t j) -> p q t j", q=2, t=PACK)
        for t in range(PACK):
            nc.scalar.activation(by_quarter(lse_lo[:, t, :]), ex_sum[:, :2, t, :], ACT.Ln)
        nc.scalar.activation(lse_hi, ex_sum[:, 2:], ACT.Ln)

        z2_rows = [sb("z2_rows%d" % k, [P, PACK, c.stop - c.start], BF16) for k, c in enumerate(CHUNKS)]
        z2_woven = [sb("z2_woven%d" % k, [P, PACK * (c.stop - c.start)], BF16) for k, c in enumerate(CHUNKS)]
        z2_codes = sb("z2_codes", [P, N], U32)
        z2_scales = sb("z2_scales", [P, N], U8)
        first_acc = [bank("first_acc%d" % k, c.stop - c.start, PACK + k) for k, c in enumerate(CHUNKS)]

        def z2_chunk(k):
            cols = CHUNKS[k]
            for t in range(PACK):
                nc.vector.scalar_tensor_tensor(
                    z2_rows[k][:, t, :], lse_lo[:, t, :] if k == 0 else lse_hi[:, k - 1, t, :],
                    gi_cols[:, t : t + 1], gb_n3[(k, t)], ALU.mult, ALU.subtract,
                )
            weave(nc.vector.tensor_copy, z2_woven[k][:], z2_rows[k][:])
            quantise(z2_codes[:, cols], z2_scales[:, cols], z2_woven[k][:])
            mx_pass(first_acc[k][:], z_codes[:, :P], z_scales[:, :P], z2_codes[:, cols], z2_scales[:, cols])

        spent = [ex_sum[:, q, LAST, :] for q in range(2)] + [ex_sum[:, q, t, :] for q in (2, 3) for t in range(PACK)]
        z2_chunk(0)
        for k in (1, 2):
            for t in range(PACK):
                n3_gather(k, t, spent[PACK * (k - 1) + t])
            z2_chunk(k)

        for k, cols in enumerate(CHUNKS):
            nc.scalar.activation(cv_win[0][:, cols], first_acc[k][:], ACT.Copy, scale=0.0625)

        def cv_step(c):
            rows = tile_columns(c, c + 1)
            acc = bank("cv_acc%d" % c, N, c)
            mx_pass(acc[:], z_codes[:, rows], z_scales[:, rows], z2_codes[:], z2_scales[:])
            nc.vector.tensor_scalar(cv_win[c][:, :N], acc[:], 0.0625, None, ALU.mult)

        cv_step(1)
        z_quantise(2, PACK, tag="z2_woven2")
        cv_step(2)
        cv_step(3)

        cv_n4 = [sb("cv_n4_%d" % c, [P, N], F32) for c in range(PACK)]
        cv_n5 = [sb("cv_n5_%d" % c, [P, N], F32) for c in range(PACK)]
        res = [sb("res%d" % c, [P, N], F32) for c in range(PACK)]
        out_rows = out.rearrange("(p c) n -> c p n", c=PACK)

        def finish(c, parts):
            top = sb("top%d" % c, [P, N], F32, tag="top")
            for cols in parts:
                nc.vector.tensor_tensor(top[:, cols], cv_n4[c][:, cols], cv_n5[c][:, cols], ALU.max)
                nc.vector.scalar_tensor_tensor(
                    res[c][:, cols], cv_win[c][:, cols], -0.75, top[:, cols], ALU.mult, ALU.add
                )
                nc.sync.dma_start(out_rows[c][:, cols], res[c][:, cols])

        for c in range(PACK):
            gather(cv_n4[c][:], cv_win[c][:], n4_l[:])
            if c < LAST:
                gather(cv_n5[c][:], cv_win[c][:], n5_l[:])
            if c > 0:
                finish(c - 1, (WHOLE,))
        for cols in (LO, HI):
            gather(cv_n5[LAST][:, cols], cv_win[LAST][:], entries(n5_l, cols.start, cols.stop))
        finish(LAST, (LO, HI))
